import numpy as np, ml_dtypes
CORES = [10,34,74,98]
N = 4
import mx_ref
BF = ml_dtypes.bfloat16
def entries(a):
    return np.ascontiguousarray(a.T).reshape(-1)
def table(e):
    return np.ascontiguousarray(np.reshape(e, (-1, 16)).T).astype(np.int32)
def f(rng, *shape):
    return mx_ref.flush((rng.standard_normal(shape, dtype=np.float32) * np.exp2(rng.integers(-2, 3, shape[:-1] + (1,)))).astype(BF))
def wide(rng, *shape, cols=0):
    v = rng.standard_normal(shape, dtype=np.float32) * np.exp2(rng.integers(-12, 13, shape)).astype(np.float32)
    if cols: v *= np.repeat(np.exp2(rng.integers(-cols, cols + 1, shape[:-2] + (1, shape[-1] // 4))) * (rng.random(shape[:-2] + (1, shape[-1] // 4)) > 0.0625), 4, axis=-1).astype(np.float32)
    return mx_ref.flush(v.astype(BF))
T, ND, CD, LM, CAPP = 1024, 64, 16, 64, 144
def lens(rng, n, total):
    a = 1 + np.minimum(LM - 1, rng.multinomial(total - n, rng.dirichlet(np.ones(n))))
    for i in rng.permutation(n): a[i] += min(LM - a[i], total - a.sum())
    return a
def places(rng, l):
    o = rng.permutation(ND); g = rng.multinomial(T - l.sum(), rng.dirichlet(np.ones(ND + 1)))
    s = np.zeros(ND, int); s[o] = np.cumsum(g[:ND]) + np.cumsum(l[o]) - l[o]
    return s
def pick(rng, l):
    p = rng.permutation(ND); a, b = p[:CD].copy(), p[CD:].copy()
    while l[a].sum() > CAPP:
        i = np.argmax(l[a]); j = rng.choice(np.flatnonzero(l[b] < l[a[i]]))
        a[i], b[j] = b[j], a[i]
    return rng.permutation(a)
def lists(rng, kind="any"):
    s, n, c = [], [], np.zeros((N, N * CD), int)
    K, J = (T - ND) // (LM - 1), (CAPP - CD) // (LM - 1)
    TT = min(T, ND // CD * CAPP)
    for q in range(N):
        d = rng.permutation(ND); l = np.ones(ND, int)
        if kind == "long": l[d[:K]] = LM
        elif kind == "full": l[d] = np.concatenate([lens(rng, CD, CAPP), lens(rng, CD, CAPP), lens(rng, ND - 2 * CD, T - 2 * CAPP)])
        elif kind == "any": l[d] = lens(rng, ND, int(rng.integers(TT - TT // 4, TT + 1)))
        s.append(table(places(rng, l))); n.append(table(l))
        for r in range(N):
            if kind == "long": e = rng.permutation(np.concatenate([rng.permutation(d[:K])[:J], rng.permutation(d[K:])[:CD - J]]))
            elif kind == "full": k = CD * int(rng.integers(0, 2)); e = rng.permutation(d[k:k + CD])
            else: e = pick(rng, l)
            c[r, CD * q:CD * q + CD] = e
    return {"st": np.stack(s), "ln": np.stack(n), "cd": np.stack([table(c[r]) for r in range(N)])}
def setup_inputs(rng):
    return {"x": f(rng, N, 128, 4 * T), "qw": f(rng, N, 128, 512), **lists(rng)}
def setup_inputs_long(rng):
    return {**setup_inputs(rng), **lists(rng, "long")}
def setup_inputs_ones(rng):
    return {**setup_inputs(rng), **lists(rng, "ones")}
def setup_inputs_full(rng):
    return {**setup_inputs(rng), **lists(rng, "full")}
def setup_inputs_below(rng):
    d = setup_inputs(rng); p = rng.permutation(N)
    s, u = rng.integers(-20, 27, N), rng.integers(-20, 28, N)
    s[p[0]] = 26; u[rng.choice(p[:-1])] = 27; s[p[-1]] = 0; u[p[-1]] = 0
    d["x"] = mx_ref.flush((-np.exp2(rng.uniform(-3, 3, (N, 128, 4 * T)) + s[:, None, None])).astype(BF))
    d["qw"] = mx_ref.flush(np.exp2(rng.uniform(-2, 2, (N, 128, 512)) + u[:, None, None]).astype(BF))
    return d
def setup_inputs_spread(rng):
    d = setup_inputs(rng); d["x"] = wide(rng, N, 128, 4 * T, cols=8); return d
def check_inputs(d):
    b = []
    L = [entries(d["ln"][r]).astype(np.int64) for r in range(N)]
    for r in range(N):
        s, l = entries(d["st"][r]).astype(np.int64), L[r]
        if l.min() < 1 or l.max() > LM: b.append("ln")
        o = np.argsort(s, kind="stable")
        if s.min() < 0 or (s + l).max() > T or (s[o][:-1] + l[o][:-1] > s[o][1:]).any(): b.append("st")
        c = entries(d["cd"][r])
        if c.min() < 0 or c.max() >= ND: b.append("cd"); continue
        for q in range(N):
            e = c[CD * q:CD * q + CD]
            if len(set(e.tolist())) != CD or L[q][e].sum() > CAPP: b.append("cd")
    return sorted(set(b))
def reference(x, qw, st, ln, cd):
    X = [mx_ref.quantize(x[q]) for q in range(N)]
    y = np.zeros((N, 128, N * CD), np.float32)
    for r in range(N):
        W = mx_ref.quantize(qw[r]); c = entries(cd[r])
        for q in range(N):
            z = mx_ref.matmul(W, X[q]); s, l = entries(st[q]), entries(ln[q])
            for i in range(CD * q, CD * q + CD):
                y[r][:, i] = z[:, s[c[i]]:s[c[i]] + l[c[i]]].max(axis=1)
    return {"y": y}

@@ -1,0 +1,299 @@
+import numpy as np
+from concourse.bass import DstId, RemoteDMATransfer
+from concourse.mybir import dt, AluOpType, ActivationFunctionType
+
+CAP = 144
+WIN = 152
+ND, CD, XC = 64, 16, 1024
+LOW = -1.0e29
+RAMP, HOLD, DROP = 8192.0, 65536.0, -262144.0
+
+SCRATCH = {
+    "xw": ("sbuf", [128, 4 * (XC + CAP)], "bfloat16"),
+    "qt": ("sbuf", [128, 512], "bfloat16"),
+    "tile": ("sbuf", [128, 4 * 4 * CAP], "bfloat16"),
+    "qwc": ("sbuf", [128, 128], "float8_e4m3fn_x4"),
+    "qws": ("sbuf", [128, 128], "uint8"),
+    "qc": ("sbuf", [128, 4 * CAP], "float8_e4m3fn_x4"),
+    "qs": ("sbuf", [128, 4 * CAP], "uint8"),
+    "lc": ("sbuf", [128, 3 * CAP], "float8_e4m3fn_x4"),
+    "lp": ("sbuf", [128, 3 * CAP], "uint8"),
+    "ps": ("psum", [128, 2048], "float32"),
+    "cdl": ("sbuf", [128, 4], "int32"),
+    "cdo": ("sbuf", [128, 8], "uint16"),
+    "lst": ("sbuf", [128, 6], "uint16"),
+    "tab": ("sbuf", [128, 8], "int32"),
+    "tdif": ("sbuf", [128, 4], "float32"),
+    "tpar": ("sbuf", [128, 4], "float32"),
+    "sel": ("sbuf", [128, 4], "float32"),
+    "lnr": ("sbuf", [128, 6], "float32"),
+    "wb": ("sbuf", [128, 128], "float32"),
+    "wn": ("sbuf", [128, 128], "float32"),
+    "nl": ("sbuf", [128, 64], "float32"),
+    "nen": ("sbuf", [128, 64], "float32"),
+    "G": ("sbuf", [128, 128], "float32"),
+    "ST": ("sbuf", [128, 160], "float32"),
+    "C": ("sbuf", [128, 128], "float32"),
+    "TR": ("sbuf", [128, 128], "float32"),
+    "J": ("sbuf", [128, 128], "float32"),
+    "cL": ("sbuf", [128, 8], "uint16"),
+    "D": ("sbuf", [128, 4 * WIN], "float32"),
+    "SS": ("sbuf", [128, 4 * CAP], "float32"),
+    "XX": ("sbuf", [128, 4 * CAP], "float32"),
+    "O": ("sbuf", [128, 4 * 36], "uint16"),
+    "wb2": ("sbuf", [128, 192], "float32"),
+    "wn2": ("sbuf", [128, 192], "float32"),
+    "G2": ("sbuf", [128, 96], "float32"),
+    "C2": ("sbuf", [128, 96], "float32"),
+    "TR2": ("sbuf", [128, 96], "float32"),
+    "seL": ("sbuf", [128, 6], "uint16"),
+    "mask": ("sbuf", [128, 4 * WIN], "float32"),
+    "Z": ("sbuf", [128, 4 * WIN], "float32"),
+    "yo": ("sbuf", [128, 64], "float32"),
+    "pi": ("sbuf", [128, 1], "int32"),
+    "lani": ("sbuf", [128, 3], "int32"),
+    "lanf": ("sbuf", [128, 3], "float32"),
+    "ul1": ("sbuf", [128, 1], "float32"),
+    "suba": ("sbuf", [128, 1], "float32"),
+    "subb": ("sbuf", [128, 1], "float32"),
+    "sub": ("sbuf", [128, 1], "float32"),
+    "u4": ("sbuf", [128, CAP], "float32"),
+    "u16": ("sbuf", [128, 96], "float32"),
+    "resm": ("sbuf", [128, 96], "float32"),
+    "A": ("sbuf", [128, CAP], "float32"),
+    "dza": ("sbuf", [128, CAP], "float32"),
+    "dz": ("sbuf", [128, CAP], "float32"),
+    "four": ("sbuf", [128, 32], "float32"),
+    "one": ("sbuf", [128, 32], "float32"),
+    "neg": ("sbuf", [128, 16], "float32"),
+}
+SEMAPHORES = ["ldcd", "ldtab", "ldqw", "ldxa", "ldxb", "v", "s", "pe", "gi", "lst0", "lst1", "lst2", "lnarr",
+              "arr0", "arr1", "arr2", "snt", "yst"]
+
+ADD, SUB, MUL, MAX = AluOpType.add, AluOpType.subtract, AluOpType.mult, AluOpType.max
+
+
+def rank_program(g, core, T, topo):
+    rank = T.rank_of(core)
+    if rank is None:
+        return
+    V, S, P, Y = g.vector, g.scalar, g.tensor, g.sync
+    Copy, Ident = ActivationFunctionType.Copy, ActivationFunctionType.Identity
+    chips = [topo.chip(c) for c in T.cores]
+    steps = sorted([1, 3, 2], key=lambda v: 1 if topo.same_plane(chips[0], chips[v]) else 0)
+    part = [rank ^ v for v in steps]
+    addr, mask, eng = [], [], []
+    for p in part:
+        a = topo.addr(T.cores[p])
+        addr.append((a[0], a[1]))
+        mask.append(topo.mask(core, T.cores[p]))
+        eng.append(len(topo.engines(core, T.cores[p])))
+
+    cnt, seen = {}, {}
+
+    def done(ins, name, n=1):
+        ins.then_inc(T.sem[name], n)
+        cnt[name] = cnt.get(name, 0) + n
+        return (name, cnt[name])
+
+    def need(qn, q, *toks):
+        for name, val in toks:
+            if seen.get((qn, name), 0) < val:
+                q.wait_ge(T.sem[name], val)
+                seen[(qn, name)] = val
+
+    def vneed(*toks):
+        need("v", V, *toks)
+
+    def v(ins):
+        return done(ins, "v")
+
+    for k in range(8):
+        q = Y if k < 4 else S
+        done(q.dma_start(T.cdl[16 * k:16 * k + 16, :], T.cd[:]), "ldcd", 16)
+    for k in range(8):
+        done(Y.dma_start(T.tab[16 * k:16 * k + 16, 4:8], T.ln[:]), "ldtab", 16)
+        done(S.dma_start(T.tab[16 * k:16 * k + 16, 0:4], T.st[:]), "ldtab", 16)
+    t_cd, t_tab = ("ldcd", 128), ("ldtab", 256)
+    t_xa = done(Y.dma_start(T.xw[:, 0:2 * XC], T.x[:, 0:2 * XC]), "ldxa", 16)
+    t_qw = done(S.dma_start(T.qt[:], T.qw[:]), "ldqw", 16)
+    need("y", Y, t_cd)
+    t_xb = done(Y.dma_start(T.xw[:, 2 * XC:4 * XC], T.x[:, 2 * XC:4 * XC]), "ldxb", 16)
+
+    i_p = done(g.iota(T.pi[:], [[0, 1]], 0, 1), "gi")
+    i_u4 = done(g.iota(T.u4[:], [[0, CAP // 4], [1, 4]], 0, 0, allow_small_or_imprecise_dtypes=True), "gi")
+    i_u16 = done(g.iota(T.u16[:], [[0, 6], [1, 16]], 0, 0, allow_small_or_imprecise_dtypes=True), "gi")
+
+    v(V.memset(T.four[:], 4.0))
+    v(V.memset(T.one[:], 1.0))
+    v(V.memset(T.neg[:], LOW))
+    t_const = v(V.memset(T.ST[:], 0.0))
+    vneed(i_p)
+    v(V.tensor_scalar(T.lani[:, 0:1], T.pi[:], 2, 3, AluOpType.arith_shift_right, AluOpType.bitwise_and))
+    v(V.tensor_scalar(T.lani[:, 1:2], T.pi[:], 3, None, AluOpType.bitwise_and))
+    t = v(V.tensor_scalar(T.lani[:, 2:3], T.pi[:], 4, 1, AluOpType.arith_shift_right, AluOpType.bitwise_and))
+    vneed(t)
+    t = v(V.tensor_copy(T.lanf[:], T.lani[:]))
+    vneed(t)
+    t_par = t
+    v(V.tensor_scalar(T.ul1[:], T.lanf[:, 0:1], 1.0, None, ADD))
+    t = v(V.tensor_scalar(T.suba[:], T.lanf[:, 0:1], 3.0, HOLD, AluOpType.is_lt, MUL))
+    vneed(t)
+    t = v(V.tensor_scalar(T.subb[:], T.lanf[:, 0:1], RAMP, T.suba[:], MUL, ADD))
+    vneed(t, i_u4)
+    t_sub = v(V.tensor_scalar(T.sub[:], T.subb[:], T.lanf[:, 1:2], None, SUB))
+    t_a = v(V.tensor_scalar(T.A[:], T.u4[:], T.ul1[:], HOLD, AluOpType.is_equal, MUL))
+    t = v(V.tensor_scalar(T.dza[:], T.u4[:], 0.0, -4.0 * RAMP, AluOpType.is_equal, MUL))
+    vneed(t, i_u16)
+    t_a = v(V.tensor_scalar(T.A[:, 0:CAP:4], T.u4[:, 0:CAP:4], 0.0, DROP, MUL, ADD))
+    t = v(V.tensor_scalar(T.dz[:], T.dza[:], RAMP + 4.0, None, ADD))
+    t_res = v(V.tensor_scalar(T.resm[:], T.u16[:], 0.0, None, AluOpType.is_gt))
+    vneed(t)
+    t_stat = v(V.memset(T.dz[:, 0:1], 0.0))
+
+    vneed(t_cd)
+    v(V.tensor_copy(T.cdo[:, 0:8:2], T.cdl[:]))
+    t_cdo = v(V.tensor_copy(T.cdo[:, 1:8:2], T.cdl[:]))
+    need("g", g, t_cdo)
+    nsent = 0
+    for s in range(3):
+        p = part[s]
+        g.remote_dma(T.lst[:, 2 * s:2 * s + 2], T.cdo[:, 2 * p:2 * p + 2], T.sem["lst%d" % s], T.sem.snt,
+                     addr[s][1], addr[s][0], mask[s])
+        nsent += eng[s]
+
+    vneed(t_tab)
+    t = v(V.tensor_tensor(T.tdif[:], T.tab[:, 1:8:2], T.tab[:, 0:8:2], SUB))
+    vneed(t)
+    t = v(V.tensor_scalar(T.tpar[:], T.tdif[:], T.lanf[:, 2:3], None, MUL))
+    vneed(t)
+    t_sel = v(V.tensor_tensor(T.sel[:], T.tpar[:], T.tab[:, 0:8:2], ADD))
+    vneed(t_sel)
+    for n in range(4):
+        t = v(V.tensor_scalar(T.wb[:, 32 * n:32 * n + 32], T.four[:] if n < 2 else T.one[:], T.sel[:, n:n + 1], None, MUL))
+    vneed(t)
+    t_wn = v(V.transpose(T.wn[:], T.wb[:]))
+    vneed(t_wn)
+    t = v(V.tensor_scalar(T.nl[:], T.wn[:, 64:128], -4.0, None, MUL))
+    vneed(t)
+    t_nen = v(V.tensor_tensor(T.nen[:], T.nl[:], T.wn[:, 0:64], SUB))
+
+    need("g", g, t_sel)
+    both = mask[0] & mask[1] & mask[2]
+    g.remote_dma_fused([RemoteDMATransfer(
+        dst_ids=[DstId(rid=a[0], pnc=a[1]) for a in addr], dma_engine_mask=both, remote_sem=T.sem.lnarr,
+        srcs=[T.sel[:, 2:4]], dsts=[T.lnr[:, 2 * s:2 * s + 2] for s in range(3)])], local_sem=T.sem.snt)
+    nsent += eng[0]
+
+    def starts(k, off, toks):
+        need("s", S, t_wn, t_const, *toks)
+        return done(S.activation(T.ST[:, 40 * k:40 * k + 32], T.wn[:, 0:64].indirect(off), Copy), "s")
+
+    def chain(k, off, toks, t_st):
+        a, c = 32 * k, CAP * k
+        vneed(t_wn, *toks)
+        t = v(V.tensor_copy(T.G[:, a:a + 32], T.wn[:, 64:128].indirect(off)))
+        vneed(t)
+        t = v(V.tensor_tensor_scan(T.C[:, a:a + 32], T.resm[:, 0:32], T.G[:, a:a + 32], 0.0, MUL, ADD))
+        vneed(t)
+        t = v(V.transpose(T.TR[:, a:a + 32], T.C[:, a:a + 32]))
+        vneed(t)
+        t_c = v(V.tensor_copy(T.cL[:, 2 * k:2 * k + 1], T.TR[:, a:a + 1]))
+        vneed(t_nen, t_st)
+        t = v(V.tensor_tensor(T.J[:, a:a + 32], T.nen[:].indirect(off), T.ST[:, 40 * k + 1:40 * k + 33], ADD))
+        vneed(t, t_c, t_d)
+        t = v(V.tensor_copy(T.D[:, WIN * k:WIN * k + CAP + 1].indirect(T.cL[:, 2 * k:2 * k + 1]), T.J[:, a:a + 16]))
+        vneed(t)
+        t = v(V.tensor_tensor_scan(T.SS[:, c:c + CAP], T.dz[:], T.D[:, WIN * k:WIN * k + CAP],
+                                   T.ST[:, 40 * k:40 * k + 1], ADD, ADD))
+        vneed(t)
+        t = v(V.tensor_tensor_scan(T.XX[:, c:c + CAP], T.A[:], T.SS[:, c:c + CAP], 0.0, ADD, MAX))
+        vneed(t)
+        return v(V.tensor_scalar(T.O[:, 36 * k:36 * k + 36], T.XX[:, c + 3:c + CAP:4], T.sub[:], None, SUB)), t_c
+
+    def piece(k, a, b):
+        return (T.tile[:, 4 * CAP * k + 16 * a:4 * CAP * k + 16 * b],
+                T.xw[:].indirect(T.O[:, 36 * k + a:36 * k + b]))
+
+    def quant(k, *toks):
+        vneed(*toks)
+        return v(V.quantize_mx(T.qc[:, CAP * k:CAP * k + CAP], T.qs[:, CAP * k:CAP * k + CAP],
+                               T.tile[:, 4 * CAP * k:4 * CAP * (k + 1)]))
+
+    t_d = v(V.memset(T.D[:], 0.0))
+    t_tail = v(V.memset(T.xw[:, 4 * XC:4 * (XC + CAP)], 0.0))
+    own = T.cdo[:, 2 * rank:2 * rank + 2]
+    t_st = starts(3, own, (t_cdo,))
+    t_o3, t_c3 = chain(3, own, (t_cdo,), t_st)
+    v(V.memset(T.mask[:], 0.0))
+    t_m = v(V.memset(T.Z[:, 0:4 * WIN:WIN], 0.0))
+    vneed(t_qw)
+    t_q = v(V.quantize_mx(T.qwc[:], T.qws[:], T.qt[:]))
+    vneed(t_m)
+    t_m3 = v(V.tensor_copy(T.mask[:, WIN * 3:WIN * 3 + CAP + 1].indirect(T.cL[:, 6:7]), T.neg[:]))
+
+    for s in range(3):
+        off = T.lst[:, 2 * s:2 * s + 2]
+        arrived = ("lst%d" % s, eng[s])
+        t_st = starts(s, off, (arrived,))
+        t_o, t_c = chain(s, off, (arrived,), t_st)
+        cut = 18 if s == 0 else 12
+        need("s", S, t_o, t_xa, t_xb, t_tail)
+        o, i = piece(s, cut, 36)
+        t_gs = done(S.activation(o, i, Copy), "s")
+        vneed(t_o, t_xa, t_xb, t_tail)
+        o, i = piece(s, 0, cut)
+        t_gv = v(V.tensor_copy(o, i))
+        t = quant(s, t_gv, t_gs)
+        need("g", g, t)
+        lo, hi = CAP * s, CAP * s + CAP
+        g.remote_dma(T.lc[:, lo:hi].bitcast(dt.uint8), T.qc[:, lo:hi].bitcast(dt.uint8), T.sem["arr%d" % s], T.sem.snt,
+                     addr[s][1], addr[s][0], mask[s])
+        g.remote_dma(T.lp[:, lo:hi], T.qs[:, lo:hi], T.sem["arr%d" % s], T.sem.snt,
+                     addr[s][1], addr[s][0], mask[s])
+        nsent += 2 * eng[s]
+
+    need("s", S, ("lnarr", sum(eng)), t_const)
+    for n in range(6):
+        t = done(S.activation(T.wb2[:, 32 * n:32 * n + 32], T.one[:], Ident, scale=T.lnr[:, n:n + 1]), "s")
+    o, i = piece(3, 0, 36)
+    need("s", S, t_o3)
+    t_g3 = done(S.activation(o, i, Copy), "s")
+    vneed(t)
+    t = v(V.transpose(T.wn2[:], T.wb2[:]))
+    vneed(t)
+    for s in range(3):
+        p = part[s]
+        t = v(V.tensor_copy(T.G2[:, 32 * s:32 * s + 32], T.wn2[:, 64 * s:64 * s + 64].indirect(T.cdo[:, 2 * p:2 * p + 2])))
+    vneed(t)
+    t = v(V.tensor_tensor_scan(T.C2[:], T.resm[:], T.G2[:], 0.0, MUL, ADD))
+    vneed(t)
+    t = v(V.transpose(T.TR2[:], T.C2[:]))
+    vneed(t)
+    t_se = v(V.tensor_copy(T.seL[:, 0:6:2], T.TR2[:, 0:96:32]))
+    vneed(t_se)
+    t_mk = []
+    for s in range(3):
+        t_mk.append(v(V.tensor_copy(T.mask[:, WIN * s:WIN * s + CAP + 1].indirect(T.seL[:, 2 * s:2 * s + 1]), T.neg[:])))
+    t_q3 = quant(3, t_g3)
+
+    need("p", P, t_q)
+    for k in (3, 0, 1, 2):
+        if k == 3:
+            need("p", P, t_q3)
+            rc, rp = T.qc[:, 3 * CAP:4 * CAP], T.qs[:, 3 * CAP:4 * CAP]
+            q, ends, t_mask = rank, T.cL[:, 6:7], t_m3
+        else:
+            need("p", P, ("arr%d" % k, 2 * eng[k]))
+            rc, rp = T.lc[:, CAP * k:CAP * k + CAP], T.lp[:, CAP * k:CAP * k + CAP]
+            q, ends, t_mask = part[k], T.seL[:, 2 * k:2 * k + 1], t_mk[k]
+        t = done(P.matmul_mx(T.ps[:, 512 * k:512 * k + CAP], T.qwc[:], T.qws[:], rc, rp, True, True), "pe")
+        vneed(t, t_mask)
+        t = v(V.tensor_tensor_scan(T.Z[:, WIN * k + 1:WIN * k + 1 + CAP], T.mask[:, WIN * k:WIN * k + CAP],
+                                   T.ps[:, 512 * k:512 * k + CAP], LOW, ADD, MAX))
+        vneed(t)
+        t = v(V.tensor_copy(T.yo[:, CD * q:CD * q + CD], T.Z[:, WIN * k:WIN * k + CAP + 1].indirect(ends)))
+        need("y", Y, t)
+        done(Y.dma_start(T.y[:, CD * q:CD * q + CD], T.yo[:, CD * q:CD * q + CD]), "yst", 16)
+    need("y", Y, ("yst", 64))
+    need("g", g, ("snt", nsent))

@@ -4,73 +4,32 @@ from concourse.mybir import dt, AluOpType, ActivationFunctionType
 
 CAP = 144
 WIN = 152
+KO = CAP // 4
 ND, CD, XC = 64, 16, 1024
 LOW = -1.0e29
 RAMP, HOLD, DROP = 8192.0, 65536.0, -262144.0
 
-SCRATCH = {
-    "xw": ("sbuf", [128, 4 * (XC + CAP)], "bfloat16"),
-    "qt": ("sbuf", [128, 512], "bfloat16"),
-    "tile": ("sbuf", [128, 4 * 4 * CAP], "bfloat16"),
-    "qwc": ("sbuf", [128, 128], "float8_e4m3fn_x4"),
-    "qws": ("sbuf", [128, 128], "uint8"),
-    "qc": ("sbuf", [128, 4 * CAP], "float8_e4m3fn_x4"),
-    "qs": ("sbuf", [128, 4 * CAP], "uint8"),
-    "lc": ("sbuf", [128, 3 * CAP], "float8_e4m3fn_x4"),
-    "lp": ("sbuf", [128, 3 * CAP], "uint8"),
-    "ps": ("psum", [128, 2048], "float32"),
-    "cdl": ("sbuf", [128, 4], "int32"),
-    "cdo": ("sbuf", [128, 8], "uint16"),
-    "lst": ("sbuf", [128, 6], "uint16"),
-    "tab": ("sbuf", [128, 8], "int32"),
-    "tdif": ("sbuf", [128, 4], "float32"),
-    "tpar": ("sbuf", [128, 4], "float32"),
-    "sel": ("sbuf", [128, 4], "float32"),
-    "lnr": ("sbuf", [128, 6], "float32"),
-    "wb": ("sbuf", [128, 128], "float32"),
-    "wn": ("sbuf", [128, 128], "float32"),
-    "nl": ("sbuf", [128, 64], "float32"),
-    "nen": ("sbuf", [128, 64], "float32"),
-    "G": ("sbuf", [128, 128], "float32"),
-    "ST": ("sbuf", [128, 160], "float32"),
-    "C": ("sbuf", [128, 128], "float32"),
-    "TR": ("sbuf", [128, 128], "float32"),
-    "J": ("sbuf", [128, 128], "float32"),
-    "cL": ("sbuf", [128, 8], "uint16"),
-    "D": ("sbuf", [128, 4 * WIN], "float32"),
-    "SS": ("sbuf", [128, 4 * CAP], "float32"),
-    "XX": ("sbuf", [128, 4 * CAP], "float32"),
-    "O": ("sbuf", [128, 4 * 36], "uint16"),
-    "wb2": ("sbuf", [128, 192], "float32"),
-    "wn2": ("sbuf", [128, 192], "float32"),
-    "G2": ("sbuf", [128, 96], "float32"),
-    "C2": ("sbuf", [128, 96], "float32"),
-    "TR2": ("sbuf", [128, 96], "float32"),
-    "seL": ("sbuf", [128, 6], "uint16"),
-    "mask": ("sbuf", [128, 4 * WIN], "float32"),
-    "Z": ("sbuf", [128, 4 * WIN], "float32"),
-    "yo": ("sbuf", [128, 64], "float32"),
-    "pi": ("sbuf", [128, 1], "int32"),
-    "lani": ("sbuf", [128, 3], "int32"),
-    "lanf": ("sbuf", [128, 3], "float32"),
-    "ul1": ("sbuf", [128, 1], "float32"),
-    "suba": ("sbuf", [128, 1], "float32"),
-    "subb": ("sbuf", [128, 1], "float32"),
-    "sub": ("sbuf", [128, 1], "float32"),
-    "u4": ("sbuf", [128, CAP], "float32"),
-    "u16": ("sbuf", [128, 96], "float32"),
-    "resm": ("sbuf", [128, 96], "float32"),
-    "A": ("sbuf", [128, CAP], "float32"),
-    "dza": ("sbuf", [128, CAP], "float32"),
-    "dz": ("sbuf", [128, CAP], "float32"),
-    "four": ("sbuf", [128, 32], "float32"),
-    "one": ("sbuf", [128, 32], "float32"),
-    "neg": ("sbuf", [128, 16], "float32"),
-}
-SEMAPHORES = ["ldcd", "ldtab", "ldqw", "ldxa", "ldxb", "v", "s", "pe", "gi", "lst0", "lst1", "lst2", "lnarr",
+F, I, U, B = "float32", "int32", "uint16", "bfloat16"
+SCRATCH = {n: ("sbuf", [128, w], d) for n, w, d in [
+    ("xw", 4 * (XC + CAP), B), ("qt", 512, B), ("tile", 16 * CAP, B),
+    ("qwc", 128, "float8_e4m3fn_x4"), ("qws", 128, "uint8"), ("qc", 4 * CAP, "float8_e4m3fn_x4"), ("qs", 4 * CAP, "uint8"),
+    ("lc", 3 * CAP, "float8_e4m3fn_x4"), ("lp", 3 * CAP, "uint8"),
+    ("cdl", 4, I), ("cds", 4, U), ("cdo", 8, U), ("lst", 12, U), ("lo", 8, U),
+    ("tab", 8, I), ("tdif", 4, F), ("tpar", 4, F), ("sel", 4, F), ("lnb", 2, B), ("lnr", 6, B),
+    ("wb", 128, F), ("wn", 128, F), ("nl", 64, F), ("nen", 64, F),
+    ("G", 128, F), ("ST", 136, F), ("C", 128, F), ("TR", 128, F), ("J", 128, F), ("cL", 8, U),
+    ("D", 4 * WIN, F), ("SS", 4 * CAP, F), ("XX", 4 * CAP, F), ("O", CAP, U),
+    ("wb2", 192, F), ("wn2", 192, F), ("G2", 96, F), ("C2", 96, F), ("TR2", 96, F), ("seL", 6, U),
+    ("mask", 4 * WIN, F), ("Z", 4 * WIN, F), ("yo", 64, F),
+    ("pi", 1, I), ("lani", 3, I), ("lanf", 3, F), ("ul1", 1, F), ("suba", 1, F), ("subb", 1, F), ("sub", 1, F),
+    ("u4", CAP, F), ("u16", 128, F), ("resm", 128, F), ("A", CAP, F), ("dza", CAP, F), ("dz", CAP, F),
+    ("four", 32, F), ("one", 32, F), ("zer", 32, F), ("neg", 16, F)]}
+SCRATCH["ps"] = ("psum", [128, 2048], F)
+SEMAPHORES = ["ldcd", "ldtab", "ldqw", "ldxa", "ldxb", "v", "s", "pe", "gi", "lst", "lnarr",
               "arr0", "arr1", "arr2", "snt", "yst"]
 
 ADD, SUB, MUL, MAX = AluOpType.add, AluOpType.subtract, AluOpType.mult, AluOpType.max
+SHR, AND, EQ = AluOpType.arith_shift_right, AluOpType.bitwise_and, AluOpType.is_equal
 
 
 def rank_program(g, core, T, topo):
@@ -88,6 +47,8 @@ def rank_program(g, core, T, topo):
         addr.append((a[0], a[1]))
         mask.append(topo.mask(core, T.cores[p]))
         eng.append(len(topo.engines(core, T.cores[p])))
+    dsts = [DstId(rid=a[0], pnc=a[1]) for a in addr]
+    both = mask[0] & mask[1] & mask[2]
 
     cnt, seen = {}, {}
 
@@ -121,56 +82,37 @@ def rank_program(g, core, T, topo):
     t_xb = done(Y.dma_start(T.xw[:, 2 * XC:4 * XC], T.x[:, 2 * XC:4 * XC]), "ldxb", 16)
 
     i_p = done(g.iota(T.pi[:], [[0, 1]], 0, 1), "gi")
-    i_u4 = done(g.iota(T.u4[:], [[0, CAP // 4], [1, 4]], 0, 0, allow_small_or_imprecise_dtypes=True), "gi")
-    i_u16 = done(g.iota(T.u16[:], [[0, 6], [1, 16]], 0, 0, allow_small_or_imprecise_dtypes=True), "gi")
-
+    i_u16 = done(g.iota(T.u16[:], [[0, 8], [1, 16]], 0, 0, allow_small_or_imprecise_dtypes=True), "gi")
+    i_u4 = done(g.iota(T.u4[:], [[0, KO], [1, 4]], 0, 0, allow_small_or_imprecise_dtypes=True), "gi")
+    vneed(i_p)
+    v(V.tensor_scalar(T.lani[:, 0:1], T.pi[:], 2, 3, SHR, AND))
+    v(V.tensor_scalar(T.lani[:, 1:2], T.pi[:], 3, None, AND))
+    t = v(V.tensor_scalar(T.lani[:, 2:3], T.pi[:], 4, 1, SHR, AND))
     v(V.memset(T.four[:], 4.0))
     v(V.memset(T.one[:], 1.0))
-    v(V.memset(T.neg[:], LOW))
-    t_const = v(V.memset(T.ST[:], 0.0))
-    vneed(i_p)
-    v(V.tensor_scalar(T.lani[:, 0:1], T.pi[:], 2, 3, AluOpType.arith_shift_right, AluOpType.bitwise_and))
-    v(V.tensor_scalar(T.lani[:, 1:2], T.pi[:], 3, None, AluOpType.bitwise_and))
-    t = v(V.tensor_scalar(T.lani[:, 2:3], T.pi[:], 4, 1, AluOpType.arith_shift_right, AluOpType.bitwise_and))
     vneed(t)
-    t = v(V.tensor_copy(T.lanf[:], T.lani[:]))
-    vneed(t)
-    t_par = t
-    v(V.tensor_scalar(T.ul1[:], T.lanf[:, 0:1], 1.0, None, ADD))
-    t = v(V.tensor_scalar(T.suba[:], T.lanf[:, 0:1], 3.0, HOLD, AluOpType.is_lt, MUL))
-    vneed(t)
-    t = v(V.tensor_scalar(T.subb[:], T.lanf[:, 0:1], RAMP, T.suba[:], MUL, ADD))
-    vneed(t, i_u4)
-    t_sub = v(V.tensor_scalar(T.sub[:], T.subb[:], T.lanf[:, 1:2], None, SUB))
-    t_a = v(V.tensor_scalar(T.A[:], T.u4[:], T.ul1[:], HOLD, AluOpType.is_equal, MUL))
-    t = v(V.tensor_scalar(T.dza[:], T.u4[:], 0.0, -4.0 * RAMP, AluOpType.is_equal, MUL))
-    vneed(t, i_u16)
-    t_a = v(V.tensor_scalar(T.A[:, 0:CAP:4], T.u4[:, 0:CAP:4], 0.0, DROP, MUL, ADD))
-    t = v(V.tensor_scalar(T.dz[:], T.dza[:], RAMP + 4.0, None, ADD))
-    t_res = v(V.tensor_scalar(T.resm[:], T.u16[:], 0.0, None, AluOpType.is_gt))
-    vneed(t)
-    t_stat = v(V.memset(T.dz[:, 0:1], 0.0))
+    v(V.tensor_copy(T.lanf[:], T.lani[:]))
+    v(V.memset(T.ST[:, 128:136], 0.0))
+    vneed(i_u16)
+    t_early = v(V.tensor_scalar(T.resm[:], T.u16[:], 0.0, None, AluOpType.is_gt))
 
     vneed(t_cd)
-    v(V.tensor_copy(T.cdo[:, 0:8:2], T.cdl[:]))
-    t_cdo = v(V.tensor_copy(T.cdo[:, 1:8:2], T.cdl[:]))
-    need("g", g, t_cdo)
-    nsent = 0
-    for s in range(3):
-        p = part[s]
-        g.remote_dma(T.lst[:, 2 * s:2 * s + 2], T.cdo[:, 2 * p:2 * p + 2], T.sem["lst%d" % s], T.sem.snt,
-                     addr[s][1], addr[s][0], mask[s])
-        nsent += eng[s]
+    t = v(V.tensor_copy(T.cds[:], T.cdl[:]))
+    need("g", g, t)
+    g.remote_dma_fused([RemoteDMATransfer(dst_ids=dsts, dma_engine_mask=both, remote_sem=T.sem.lst, srcs=[T.cds[:]],
+                                          dsts=[T.lst[:, 4 * s:4 * s + 4] for s in range(3)])], local_sem=T.sem.snt)
+    nsent = eng[0]
 
-    vneed(t_tab)
+    vneed(t_tab, t_early)
     t = v(V.tensor_tensor(T.tdif[:], T.tab[:, 1:8:2], T.tab[:, 0:8:2], SUB))
     vneed(t)
     t = v(V.tensor_scalar(T.tpar[:], T.tdif[:], T.lanf[:, 2:3], None, MUL))
     vneed(t)
-    t_sel = v(V.tensor_tensor(T.sel[:], T.tpar[:], T.tab[:, 0:8:2], ADD))
-    vneed(t_sel)
+    t = v(V.tensor_tensor(T.sel[:], T.tpar[:], T.tab[:, 0:8:2], ADD))
+    vneed(t)
     for n in range(4):
         t = v(V.tensor_scalar(T.wb[:, 32 * n:32 * n + 32], T.four[:] if n < 2 else T.one[:], T.sel[:, n:n + 1], None, MUL))
+    t_lnb = v(V.tensor_copy(T.lnb[:], T.sel[:, 2:4]))
     vneed(t)
     t_wn = v(V.transpose(T.wn[:], T.wb[:]))
     vneed(t_wn)
@@ -178,95 +120,116 @@ def rank_program(g, core, T, topo):
     vneed(t)
     t_nen = v(V.tensor_tensor(T.nen[:], T.nl[:], T.wn[:, 0:64], SUB))
 
-    need("g", g, t_sel)
-    both = mask[0] & mask[1] & mask[2]
-    g.remote_dma_fused([RemoteDMATransfer(
-        dst_ids=[DstId(rid=a[0], pnc=a[1]) for a in addr], dma_engine_mask=both, remote_sem=T.sem.lnarr,
-        srcs=[T.sel[:, 2:4]], dsts=[T.lnr[:, 2 * s:2 * s + 2] for s in range(3)])], local_sem=T.sem.snt)
+    need("g", g, t_lnb)
+    g.remote_dma_fused([RemoteDMATransfer(dst_ids=dsts, dma_engine_mask=both, remote_sem=T.sem.lnarr, srcs=[T.lnb[:]],
+                                          dsts=[T.lnr[:, 2 * s:2 * s + 2] for s in range(3)])], local_sem=T.sem.snt)
     nsent += eng[0]
 
-    def starts(k, off, toks):
-        need("s", S, t_wn, t_const, *toks)
-        return done(S.activation(T.ST[:, 40 * k:40 * k + 32], T.wn[:, 0:64].indirect(off), Copy), "s")
+    v(V.tensor_copy(T.lo[:, 6:7], T.cdl[:, rank:rank + 1]))
+    v(V.tensor_copy(T.lo[:, 7:8], T.cdl[:, rank:rank + 1]))
+    t_d = v(V.memset(T.D[:], 0.0))
+    vneed(i_u4)
+    v(V.tensor_scalar(T.ul1[:], T.lanf[:, 0:1], 1.0, None, ADD))
+    v(V.tensor_scalar(T.suba[:], T.lanf[:, 0:1], 3.0, HOLD, AluOpType.is_lt, MUL))
+    t = v(V.tensor_scalar(T.dza[:], T.u4[:], 0.0, -4.0 * RAMP, EQ, MUL))
+    vneed(t)
+    v(V.tensor_scalar(T.subb[:], T.lanf[:, 0:1], RAMP, T.suba[:], MUL, ADD))
+    v(V.tensor_scalar(T.A[:], T.u4[:], T.ul1[:], HOLD, EQ, MUL))
+    t = v(V.tensor_scalar(T.dz[:], T.dza[:], RAMP + 4.0, None, ADD))
+    vneed(t)
+    v(V.tensor_scalar(T.sub[:], T.subb[:], T.lanf[:, 1:2], None, SUB))
+    v(V.tensor_scalar(T.A[:, 0:CAP:4], T.u4[:, 0:CAP:4], 0.0, DROP, MUL, ADD))
+    v(V.memset(T.dz[:, 0:1], 0.0))
+    t_tail = v(V.memset(T.xw[:, 4 * XC:4 * (XC + CAP)], 0.0))
 
-    def chain(k, off, toks, t_st):
+    vneed(("lst", sum(eng)))
+    v(V.tensor_copy(T.lo[:, 0:6:2], T.lst[:, rank:12:4]))
+    t_lo = v(V.tensor_copy(T.lo[:, 1:6:2], T.lst[:, rank:12:4]))
+    need("s", S, t_lo)
+    t_st = done(S.activation(T.ST[:, 0:128], T.wn[:, 0:64].indirect(T.lo[:]), Copy), "s")
+    vneed(t_lo)
+    t = v(V.tensor_copy(T.G[:], T.wn[:, 64:128].indirect(T.lo[:])))
+    vneed(t)
+    t = v(V.tensor_tensor_scan(T.C[:], T.resm[:], T.G[:], 0.0, MUL, ADD))
+    vneed(t)
+    t = v(V.transpose(T.TR[:], T.C[:]))
+    vneed(t)
+    t_c = v(V.tensor_copy(T.cL[:, 0:8:2], T.TR[:, 0:128:32]))
+    vneed(t_st)
+    t_j = v(V.tensor_tensor(T.J[:], T.nen[:].indirect(T.lo[:]), T.ST[:, 1:129], ADD))
+
+    def chain(k):
         a, c = 32 * k, CAP * k
-        vneed(t_wn, *toks)
-        t = v(V.tensor_copy(T.G[:, a:a + 32], T.wn[:, 64:128].indirect(off)))
-        vneed(t)
-        t = v(V.tensor_tensor_scan(T.C[:, a:a + 32], T.resm[:, 0:32], T.G[:, a:a + 32], 0.0, MUL, ADD))
-        vneed(t)
-        t = v(V.transpose(T.TR[:, a:a + 32], T.C[:, a:a + 32]))
-        vneed(t)
-        t_c = v(V.tensor_copy(T.cL[:, 2 * k:2 * k + 1], T.TR[:, a:a + 1]))
-        vneed(t_nen, t_st)
-        t = v(V.tensor_tensor(T.J[:, a:a + 32], T.nen[:].indirect(off), T.ST[:, 40 * k + 1:40 * k + 33], ADD))
-        vneed(t, t_c, t_d)
+        vneed(t_j, t_c, t_d, t_tail)
         t = v(V.tensor_copy(T.D[:, WIN * k:WIN * k + CAP + 1].indirect(T.cL[:, 2 * k:2 * k + 1]), T.J[:, a:a + 16]))
         vneed(t)
-        t = v(V.tensor_tensor_scan(T.SS[:, c:c + CAP], T.dz[:], T.D[:, WIN * k:WIN * k + CAP],
-                                   T.ST[:, 40 * k:40 * k + 1], ADD, ADD))
+        t = v(V.tensor_tensor_scan(T.SS[:, c:c + CAP], T.dz[:], T.D[:, WIN * k:WIN * k + CAP], T.ST[:, a:a + 1], ADD, ADD))
         vneed(t)
         t = v(V.tensor_tensor_scan(T.XX[:, c:c + CAP], T.A[:], T.SS[:, c:c + CAP], 0.0, ADD, MAX))
         vneed(t)
-        return v(V.tensor_scalar(T.O[:, 36 * k:36 * k + 36], T.XX[:, c + 3:c + CAP:4], T.sub[:], None, SUB)), t_c
+        return v(V.tensor_scalar(T.O[:, KO * k:KO * k + KO], T.XX[:, c + 3:c + CAP:4], T.sub[:], None, SUB))
 
     def piece(k, a, b):
-        return (T.tile[:, 4 * CAP * k + 16 * a:4 * CAP * k + 16 * b],
-                T.xw[:].indirect(T.O[:, 36 * k + a:36 * k + b]))
+        return (T.tile[:, 4 * CAP * k + 16 * a:4 * CAP * k + 16 * b], T.xw[:].indirect(T.O[:, KO * k + a:KO * k + b]))
+
+    def gather_s(k, cut, t_o):
+        need("s", S, t_o, t_xa, t_xb)
+        o, i = piece(k, cut, KO)
+        return done(S.activation(o, i, Copy), "s")
+
+    def gather_v(k, cut, t_o):
+        vneed(t_o, t_xa, t_xb)
+        o, i = piece(k, 0, cut)
+        return v(V.tensor_copy(o, i))
 
     def quant(k, *toks):
         vneed(*toks)
         return v(V.quantize_mx(T.qc[:, CAP * k:CAP * k + CAP], T.qs[:, CAP * k:CAP * k + CAP],
                                T.tile[:, 4 * CAP * k:4 * CAP * (k + 1)]))
 
-    t_d = v(V.memset(T.D[:], 0.0))
-    t_tail = v(V.memset(T.xw[:, 4 * XC:4 * (XC + CAP)], 0.0))
-    own = T.cdo[:, 2 * rank:2 * rank + 2]
-    t_st = starts(3, own, (t_cdo,))
-    t_o3, t_c3 = chain(3, own, (t_cdo,), t_st)
-    v(V.memset(T.mask[:], 0.0))
-    t_m = v(V.memset(T.Z[:, 0:4 * WIN:WIN], 0.0))
-    vneed(t_qw)
-    t_q = v(V.quantize_mx(T.qwc[:], T.qws[:], T.qt[:]))
-    vneed(t_m)
-    t_m3 = v(V.tensor_copy(T.mask[:, WIN * 3:WIN * 3 + CAP + 1].indirect(T.cL[:, 6:7]), T.neg[:]))
-
-    for s in range(3):
-        off = T.lst[:, 2 * s:2 * s + 2]
-        arrived = ("lst%d" % s, eng[s])
-        t_st = starts(s, off, (arrived,))
-        t_o, t_c = chain(s, off, (arrived,), t_st)
-        cut = 18 if s == 0 else 12
-        need("s", S, t_o, t_xa, t_xb, t_tail)
-        o, i = piece(s, cut, 36)
-        t_gs = done(S.activation(o, i, Copy), "s")
-        vneed(t_o, t_xa, t_xb, t_tail)
-        o, i = piece(s, 0, cut)
-        t_gv = v(V.tensor_copy(o, i))
-        t = quant(s, t_gv, t_gs)
+    def send(s, t):
         need("g", g, t)
         lo, hi = CAP * s, CAP * s + CAP
         g.remote_dma(T.lc[:, lo:hi].bitcast(dt.uint8), T.qc[:, lo:hi].bitcast(dt.uint8), T.sem["arr%d" % s], T.sem.snt,
                      addr[s][1], addr[s][0], mask[s])
         g.remote_dma(T.lp[:, lo:hi], T.qs[:, lo:hi], T.sem["arr%d" % s], T.sem.snt,
                      addr[s][1], addr[s][0], mask[s])
-        nsent += 2 * eng[s]
+        return 2 * eng[s]
 
-    need("s", S, ("lnarr", sum(eng)), t_const)
+    t_o = chain(0)
+    t_s = gather_s(0, 18, t_o)
+    t_v = gather_v(0, 18, t_o)
+    nsent += send(0, quant(0, t_v, t_s))
+    t_o = chain(1)
+    t_s = gather_s(1, 0, t_o)
+    t_o = chain(2)
+    t_s2 = gather_s(2, 18, t_o)
+    nsent += send(1, quant(1, t_s))
+    t_v = gather_v(2, 18, t_o)
+    nsent += send(2, quant(2, t_v, t_s2))
+
+    t_o = chain(3)
+    v(V.memset(T.zer[:], 0.0))
+    v(V.memset(T.neg[:], LOW))
+    v(V.tensor_copy(T.cdo[:, 0:8:2], T.cdl[:]))
+    v(V.tensor_copy(T.cdo[:, 1:8:2], T.cdl[:]))
+    v(V.memset(T.mask[:], 0.0))
+    t_z = v(V.memset(T.Z[:, 0:4 * WIN:WIN], 0.0))
+    vneed(t_qw)
+    t_q = v(V.quantize_mx(T.qwc[:], T.qws[:], T.qt[:]))
+    need("s", S, ("lnarr", sum(eng)), t_z)
     for n in range(6):
-        t = done(S.activation(T.wb2[:, 32 * n:32 * n + 32], T.one[:], Ident, scale=T.lnr[:, n:n + 1]), "s")
-    o, i = piece(3, 0, 36)
-    need("s", S, t_o3)
-    t_g3 = done(S.activation(o, i, Copy), "s")
-    vneed(t)
+        t = done(S.activation(T.wb2[:, 32 * n:32 * n + 32], T.zer[:], Ident, bias=T.lnr[:, n:n + 1]), "s")
+    t_g3 = gather_s(3, 0, t_o)
+    vneed(t, t_z)
+    t_m3 = v(V.tensor_copy(T.mask[:, WIN * 3:WIN * 3 + CAP + 1].indirect(T.cL[:, 6:7]), T.neg[:]))
     t = v(V.transpose(T.wn2[:], T.wb2[:]))
     vneed(t)
     for s in range(3):
         p = part[s]
         t = v(V.tensor_copy(T.G2[:, 32 * s:32 * s + 32], T.wn2[:, 64 * s:64 * s + 64].indirect(T.cdo[:, 2 * p:2 * p + 2])))
     vneed(t)
-    t = v(V.tensor_tensor_scan(T.C2[:], T.resm[:], T.G2[:], 0.0, MUL, ADD))
+    t = v(V.tensor_tensor_scan(T.C2[:], T.resm[:, 0:96], T.G2[:], 0.0, MUL, ADD))
     vneed(t)
     t = v(V.transpose(T.TR2[:], T.C2[:]))
     vneed(t)

@@ -6,6 +6,7 @@ CAP = 144
 WIN = 152
 KO = CAP // 4
 ND, CD, XC = 64, 16, 1024
+XA = 1408
 LOW = -1.0e29
 RAMP, HOLD, DROP = 8192.0, 65536.0, -262144.0
 
@@ -15,17 +16,17 @@ SCRATCH = {n: ("sbuf", [128, w], d) for n, w, d in [
     ("qwc", 128, "float8_e4m3fn_x4"), ("qws", 128, "uint8"), ("qc", 4 * CAP, "float8_e4m3fn_x4"), ("qs", 4 * CAP, "uint8"),
     ("lc", 3 * CAP, "float8_e4m3fn_x4"), ("lp", 3 * CAP, "uint8"),
     ("cdl", 4, I), ("cds", 4, U), ("cdo", 8, U), ("lst", 12, U), ("lo", 8, U),
-    ("tab", 8, I), ("tdif", 4, F), ("tpar", 4, F), ("sel", 4, F), ("lnb", 2, B), ("lnr", 6, B),
-    ("wb", 128, F), ("wn", 128, F), ("nl", 64, F), ("nen", 64, F),
+    ("row", 128, I), ("bc", 128, I), ("lnt", 64, F), ("lnb", 2, B), ("lnr", 6, B),
+    ("wn", 128, F), ("nl", 64, F), ("nen", 64, F),
     ("G", 128, F), ("ST", 136, F), ("C", 128, F), ("TR", 128, F), ("J", 128, F), ("cL", 8, U),
     ("D", 4 * WIN, F), ("SS", 4 * CAP, F), ("XX", 4 * CAP, F), ("O", CAP, U),
     ("wb2", 192, F), ("wn2", 192, F), ("G2", 96, F), ("C2", 96, F), ("TR2", 96, F), ("seL", 6, U),
     ("mask", 4 * WIN, F), ("Z", 4 * WIN, F), ("yo", 64, F),
-    ("pi", 1, I), ("lani", 3, I), ("lanf", 3, F), ("ul1", 1, F), ("suba", 1, F), ("subb", 1, F), ("sub", 1, F),
+    ("pi", 1, I), ("lani", 2, I), ("lanf", 2, F), ("ul1", 1, F), ("suba", 1, F), ("subb", 1, F), ("sub", 1, F),
     ("u4", CAP, F), ("u16", 128, F), ("resm", 128, F), ("A", CAP, F), ("dza", CAP, F), ("dz", CAP, F),
-    ("four", 32, F), ("one", 32, F), ("zer", 32, F), ("neg", 16, F)]}
+    ("zer", 32, F), ("neg", 16, F)]}
 SCRATCH["ps"] = ("psum", [128, 2048], F)
-SEMAPHORES = ["ldcd", "ldtab", "ldqw", "ldxa", "ldxb", "v", "s", "pe", "gi", "lst", "lnarr",
+SEMAPHORES = ["ldcd", "ldtab", "ldqw", "ldxa", "ldxb", "v", "s", "pe", "gi", "go", "lst", "lnarr",
               "arr0", "arr1", "arr2", "snt", "yst"]
 
 ADD, SUB, MUL, MAX = AluOpType.add, AluOpType.subtract, AluOpType.mult, AluOpType.max
@@ -41,12 +42,12 @@ def rank_program(g, core, T, topo):
     chips = [topo.chip(c) for c in T.cores]
     steps = sorted([1, 3, 2], key=lambda v: 1 if topo.same_plane(chips[0], chips[v]) else 0)
     part = [rank ^ v for v in steps]
-    addr, mask, eng = [], [], []
+    addr, mask, ne = [], [], []
     for p in part:
         a = topo.addr(T.cores[p])
         addr.append((a[0], a[1]))
         mask.append(topo.mask(core, T.cores[p]))
-        eng.append(len(topo.engines(core, T.cores[p])))
+        ne.append(len(topo.engines(core, T.cores[p])))
     dsts = [DstId(rid=a[0], pnc=a[1]) for a in addr]
     both = mask[0] & mask[1] & mask[2]
 
@@ -72,63 +73,24 @@ def rank_program(g, core, T, topo):
     for k in range(8):
         q = Y if k < 4 else S
         done(q.dma_start(T.cdl[16 * k:16 * k + 16, :], T.cd[:]), "ldcd", 16)
-    for k in range(8):
-        done(Y.dma_start(T.tab[16 * k:16 * k + 16, 4:8], T.ln[:]), "ldtab", 16)
-        done(S.dma_start(T.tab[16 * k:16 * k + 16, 0:4], T.st[:]), "ldtab", 16)
-    t_cd, t_tab = ("ldcd", 128), ("ldtab", 256)
-    t_xa = done(Y.dma_start(T.xw[:, 0:2 * XC], T.x[:, 0:2 * XC]), "ldxa", 16)
-    t_qw = done(S.dma_start(T.qt[:], T.qw[:]), "ldqw", 16)
-    need("y", Y, t_cd)
-    t_xb = done(Y.dma_start(T.xw[:, 2 * XC:4 * XC], T.x[:, 2 * XC:4 * XC]), "ldxb", 16)
+    done(S.dma_start(T.row[0:1, 0:64], T.st[:]), "ldtab", 16)
+    done(S.dma_start(T.row[0:1, 64:128], T.ln[:]), "ldtab", 16)
+    t_cd, t_tab = ("ldcd", 128), ("ldtab", 32)
+    t_xa = done(Y.dma_start(T.xw[:, 0:XA], T.x[:, 0:XA]), "ldxa", 16)
+    Y.wait_ge(T.sem.go, 1)
+    t_xb = done(Y.dma_start(T.xw[:, XA:4 * XC], T.x[:, XA:4 * XC]), "ldxb", 16)
+    t_qw = done(Y.dma_start(T.qt[:], T.qw[:]), "ldqw", 16)
 
     i_p = done(g.iota(T.pi[:], [[0, 1]], 0, 1), "gi")
-    i_u16 = done(g.iota(T.u16[:], [[0, 8], [1, 16]], 0, 0, allow_small_or_imprecise_dtypes=True), "gi")
     i_u4 = done(g.iota(T.u4[:], [[0, KO], [1, 4]], 0, 0, allow_small_or_imprecise_dtypes=True), "gi")
+    i_u16 = done(g.iota(T.u16[:], [[0, 8], [1, 16]], 0, 0, allow_small_or_imprecise_dtypes=True), "gi")
     vneed(i_p)
     v(V.tensor_scalar(T.lani[:, 0:1], T.pi[:], 2, 3, SHR, AND))
-    v(V.tensor_scalar(T.lani[:, 1:2], T.pi[:], 3, None, AND))
-    t = v(V.tensor_scalar(T.lani[:, 2:3], T.pi[:], 4, 1, SHR, AND))
-    v(V.memset(T.four[:], 4.0))
-    v(V.memset(T.one[:], 1.0))
-    vneed(t)
-    v(V.tensor_copy(T.lanf[:], T.lani[:]))
+    t = v(V.tensor_scalar(T.lani[:, 1:2], T.pi[:], 3, None, AND))
     v(V.memset(T.ST[:, 128:136], 0.0))
-    vneed(i_u16)
-    t_early = v(V.tensor_scalar(T.resm[:], T.u16[:], 0.0, None, AluOpType.is_gt))
-
-    vneed(t_cd)
-    t = v(V.tensor_copy(T.cds[:], T.cdl[:]))
-    need("g", g, t)
-    g.remote_dma_fused([RemoteDMATransfer(dst_ids=dsts, dma_engine_mask=both, remote_sem=T.sem.lst, srcs=[T.cds[:]],
-                                          dsts=[T.lst[:, 4 * s:4 * s + 4] for s in range(3)])], local_sem=T.sem.snt)
-    nsent = eng[0]
-
-    vneed(t_tab, t_early)
-    t = v(V.tensor_tensor(T.tdif[:], T.tab[:, 1:8:2], T.tab[:, 0:8:2], SUB))
     vneed(t)
-    t = v(V.tensor_scalar(T.tpar[:], T.tdif[:], T.lanf[:, 2:3], None, MUL))
-    vneed(t)
-    t = v(V.tensor_tensor(T.sel[:], T.tpar[:], T.tab[:, 0:8:2], ADD))
-    vneed(t)
-    for n in range(4):
-        t = v(V.tensor_scalar(T.wb[:, 32 * n:32 * n + 32], T.four[:] if n < 2 else T.one[:], T.sel[:, n:n + 1], None, MUL))
-    t_lnb = v(V.tensor_copy(T.lnb[:], T.sel[:, 2:4]))
-    vneed(t)
-    t_wn = v(V.transpose(T.wn[:], T.wb[:]))
-    vneed(t_wn)
-    t = v(V.tensor_scalar(T.nl[:], T.wn[:, 64:128], -4.0, None, MUL))
-    vneed(t)
-    t_nen = v(V.tensor_tensor(T.nen[:], T.nl[:], T.wn[:, 0:64], SUB))
-
-    need("g", g, t_lnb)
-    g.remote_dma_fused([RemoteDMATransfer(dst_ids=dsts, dma_engine_mask=both, remote_sem=T.sem.lnarr, srcs=[T.lnb[:]],
-                                          dsts=[T.lnr[:, 2 * s:2 * s + 2] for s in range(3)])], local_sem=T.sem.snt)
-    nsent += eng[0]
-
-    v(V.tensor_copy(T.lo[:, 6:7], T.cdl[:, rank:rank + 1]))
-    v(V.tensor_copy(T.lo[:, 7:8], T.cdl[:, rank:rank + 1]))
-    t_d = v(V.memset(T.D[:], 0.0))
-    vneed(i_u4)
+    t = v(V.tensor_copy(T.lanf[:], T.lani[:]))
+    vneed(t, i_u4)
     v(V.tensor_scalar(T.ul1[:], T.lanf[:, 0:1], 1.0, None, ADD))
     v(V.tensor_scalar(T.suba[:], T.lanf[:, 0:1], 3.0, HOLD, AluOpType.is_lt, MUL))
     t = v(V.tensor_scalar(T.dza[:], T.u4[:], 0.0, -4.0 * RAMP, EQ, MUL))
@@ -136,13 +98,51 @@ def rank_program(g, core, T, topo):
     v(V.tensor_scalar(T.subb[:], T.lanf[:, 0:1], RAMP, T.suba[:], MUL, ADD))
     v(V.tensor_scalar(T.A[:], T.u4[:], T.ul1[:], HOLD, EQ, MUL))
     t = v(V.tensor_scalar(T.dz[:], T.dza[:], RAMP + 4.0, None, ADD))
-    vneed(t)
+    vneed(t, i_u16)
     v(V.tensor_scalar(T.sub[:], T.subb[:], T.lanf[:, 1:2], None, SUB))
     v(V.tensor_scalar(T.A[:, 0:CAP:4], T.u4[:, 0:CAP:4], 0.0, DROP, MUL, ADD))
     v(V.memset(T.dz[:, 0:1], 0.0))
-    t_tail = v(V.memset(T.xw[:, 4 * XC:4 * (XC + CAP)], 0.0))
+    t_const = v(V.tensor_scalar(T.resm[:], T.u16[:], 0.0, None, AluOpType.is_gt))
 
-    vneed(("lst", sum(eng)))
+    vneed(t_cd)
+    t = v(V.tensor_copy(T.cds[:], T.cdl[:]))
+    need("g", g, t)
+    g.remote_dma_fused([RemoteDMATransfer(dst_ids=dsts, dma_engine_mask=both, remote_sem=T.sem.lst, srcs=[T.cds[:]],
+                                          dsts=[T.lst[:, 4 * s:4 * s + 4] for s in range(3)])], local_sem=T.sem.snt)
+    nsent = ne[0]
+    g.sem_inc(T.sem.go, 1)
+    need("g", g, t_tab)
+    i_bc = done(g.partition_broadcast(T.bc[:], T.row[0:1, :], 128), "gi")
+
+    v(V.tensor_copy(T.lo[:, 6:7], T.cdl[:, rank:rank + 1]))
+    v(V.tensor_copy(T.lo[:, 7:8], T.cdl[:, rank:rank + 1]))
+    t_d = v(V.memset(T.D[:], 0.0))
+
+    vneed(i_bc)
+    for h in range(4):
+        t = v(V.tensor_copy(T.wn[:, 64 + 16 * h:80 + 16 * h], T.bc[:, 64 + h:128:4]))
+    for h in range(4):
+        t_wn = v(V.tensor_scalar(T.wn[:, 16 * h:16 + 16 * h], T.bc[:, h:64:4], 4.0, None, MUL))
+    vneed(t)
+    t = v(V.transpose(T.lnt[:], T.wn[:, 64:128]))
+    t_nl = v(V.tensor_scalar(T.nl[:], T.wn[:, 64:128], -4.0, None, MUL))
+    vneed(t)
+    t_lnb = v(V.tensor_copy(T.lnb[:], T.lnt[:, 0:64:32]))
+    vneed(t_wn, t_nl)
+    t_nen = v(V.tensor_tensor(T.nen[:], T.nl[:], T.wn[:, 0:64], SUB))
+
+    need("g", g, t_lnb)
+    g.remote_dma_fused([RemoteDMATransfer(dst_ids=dsts, dma_engine_mask=both, remote_sem=T.sem.lnarr, srcs=[T.lnb[:]],
+                                          dsts=[T.lnr[:, 2 * s:2 * s + 2] for s in range(3)])], local_sem=T.sem.snt)
+    nsent += ne[0]
+
+    t_tail = v(V.memset(T.xw[:, 4 * XC:4 * (XC + CAP)], 0.0))
+    v(V.memset(T.zer[:], 0.0))
+    v(V.memset(T.neg[:], LOW))
+    v(V.memset(T.Z[:, 0:4 * WIN:WIN], 0.0))
+    t_z = v(V.memset(T.mask[:], 0.0))
+
+    vneed(("lst", sum(ne)))
     v(V.tensor_copy(T.lo[:, 0:6:2], T.lst[:, rank:12:4]))
     t_lo = v(V.tensor_copy(T.lo[:, 1:6:2], T.lst[:, rank:12:4]))
     need("s", S, t_lo)
@@ -194,34 +194,24 @@ def rank_program(g, core, T, topo):
                      addr[s][1], addr[s][0], mask[s])
         g.remote_dma(T.lp[:, lo:hi], T.qs[:, lo:hi], T.sem["arr%d" % s], T.sem.snt,
                      addr[s][1], addr[s][0], mask[s])
-        return 2 * eng[s]
+        return 2 * ne[s]
 
-    t_o = chain(0)
-    t_s = gather_s(0, 18, t_o)
-    t_v = gather_v(0, 18, t_o)
-    nsent += send(0, quant(0, t_v, t_s))
-    t_o = chain(1)
-    t_s = gather_s(1, 0, t_o)
-    t_o = chain(2)
-    t_s2 = gather_s(2, 18, t_o)
-    nsent += send(1, quant(1, t_s))
-    t_v = gather_v(2, 18, t_o)
-    nsent += send(2, quant(2, t_v, t_s2))
+    t_o = [chain(0), chain(1), chain(2)]
+    for s in range(3):
+        t_s = gather_s(s, 18, t_o[s])
+        t_v = gather_v(s, 18, t_o[s])
+        nsent += send(s, quant(s, t_v, t_s))
 
-    t_o = chain(3)
-    v(V.memset(T.zer[:], 0.0))
-    v(V.memset(T.neg[:], LOW))
+    t_o3 = chain(3)
     v(V.tensor_copy(T.cdo[:, 0:8:2], T.cdl[:]))
-    v(V.tensor_copy(T.cdo[:, 1:8:2], T.cdl[:]))
-    v(V.memset(T.mask[:], 0.0))
-    t_z = v(V.memset(T.Z[:, 0:4 * WIN:WIN], 0.0))
+    t_cdo = v(V.tensor_copy(T.cdo[:, 1:8:2], T.cdl[:]))
     vneed(t_qw)
     t_q = v(V.quantize_mx(T.qwc[:], T.qws[:], T.qt[:]))
-    need("s", S, ("lnarr", sum(eng)), t_z)
+    need("s", S, ("lnarr", sum(ne)), t_z)
     for n in range(6):
         t = done(S.activation(T.wb2[:, 32 * n:32 * n + 32], T.zer[:], Ident, bias=T.lnr[:, n:n + 1]), "s")
-    t_g3 = gather_s(3, 0, t_o)
-    vneed(t, t_z)
+    t_g3 = gather_s(3, 0, t_o3)
+    vneed(t, t_cdo, t_z)
     t_m3 = v(V.tensor_copy(T.mask[:, WIN * 3:WIN * 3 + CAP + 1].indirect(T.cL[:, 6:7]), T.neg[:]))
     t = v(V.transpose(T.wn2[:], T.wb2[:]))
     vneed(t)
@@ -247,7 +237,7 @@ def rank_program(g, core, T, topo):
             rc, rp = T.qc[:, 3 * CAP:4 * CAP], T.qs[:, 3 * CAP:4 * CAP]
             q, ends, t_mask = rank, T.cL[:, 6:7], t_m3
         else:
-            need("p", P, ("arr%d" % k, 2 * eng[k]))
+            need("p", P, ("arr%d" % k, 2 * ne[k]))
             rc, rp = T.lc[:, CAP * k:CAP * k + CAP], T.lp[:, CAP * k:CAP * k + CAP]
             q, ends, t_mask = part[k], T.seL[:, 2 * k:2 * k + 1], t_mk[k]
         t = done(P.matmul_mx(T.ps[:, 512 * k:512 * k + CAP], T.qwc[:], T.qws[:], rc, rp, True, True), "pe")

@@ -7,30 +7,31 @@ WIN = 152
 KO = CAP // 4
 ND, CD, XC = 64, 16, 1024
 XA = 1408
+CUT = 16
 LOW = -1.0e29
-RAMP, HOLD, DROP = 8192.0, 65536.0, -262144.0
+HOLD = 8192
 
 F, I, U, B = "float32", "int32", "uint16", "bfloat16"
 SCRATCH = {n: ("sbuf", [128, w], d) for n, w, d in [
     ("xw", 4 * (XC + CAP), B), ("qt", 512, B), ("tile", 16 * CAP, B),
     ("qwc", 128, "float8_e4m3fn_x4"), ("qws", 128, "uint8"), ("qc", 4 * CAP, "float8_e4m3fn_x4"), ("qs", 4 * CAP, "uint8"),
     ("lc", 3 * CAP, "float8_e4m3fn_x4"), ("lp", 3 * CAP, "uint8"),
-    ("cdl", 4, I), ("cds", 4, U), ("cdo", 8, U), ("lst", 12, U), ("lo", 8, U),
-    ("row", 128, I), ("bc", 128, I), ("lnt", 64, F), ("lnb", 2, B), ("lnr", 6, B),
-    ("wn", 128, F), ("nl", 64, F), ("nen", 64, F),
-    ("G", 128, F), ("ST", 136, F), ("C", 128, F), ("TR", 128, F), ("J", 128, F), ("cL", 8, U),
+    ("cdl", 4, I), ("cds", 4, U), ("lst", 12, U), ("lo", 4, U),
+    ("row", 128, I), ("bc", 128, I), ("stw", 64, F), ("lnw", 64, F), ("nl", 64, F), ("nen", 64, F),
+    ("MG", 64, F), ("C", 64, F), ("ST", 72, F), ("J", 64, F), ("cL", 8, U), ("seL", 6, U),
     ("D", 4 * WIN, F), ("SS", 4 * CAP, F), ("XX", 4 * CAP, F), ("O", CAP, U),
-    ("wb2", 192, F), ("wn2", 192, F), ("G2", 96, F), ("C2", 96, F), ("TR2", 96, F), ("seL", 6, U),
-    ("mask", 4 * WIN, F), ("Z", 4 * WIN, F), ("yo", 64, F),
-    ("pi", 1, I), ("lani", 2, I), ("lanf", 2, F), ("ul1", 1, F), ("suba", 1, F), ("subb", 1, F), ("sub", 1, F),
-    ("u4", CAP, F), ("u16", 128, F), ("resm", 128, F), ("A", CAP, F), ("dza", CAP, F), ("dz", CAP, F),
-    ("zer", 32, F), ("neg", 16, F)]}
+    ("mask", 4 * WIN, F), ("Z", 4 * WIN, F), ("yo", 64, F), ("neg", 16, F),
+    ("lrow", 96, F), ("lcol", 96, F), ("u16", 64, F), ("u4", CAP, F), ("pc", 8, F), ("po", 8, U),
+    ("tri", 64, F), ("resm", 64, F), ("A", CAP, F), ("four", CAP, F)]}
 SCRATCH["ps"] = ("psum", [128, 2048], F)
-SEMAPHORES = ["ldcd", "ldtab", "ldqw", "ldxa", "ldxb", "v", "s", "pe", "gi", "go", "lst", "lnarr",
+SEMAPHORES = ["ldcd", "ldtab", "ldqw", "ldxa", "ldxb", "v", "s", "pe", "gi", "go", "lst", "sel",
               "arr0", "arr1", "arr2", "snt", "yst"]
 
-ADD, SUB, MUL, MAX = AluOpType.add, AluOpType.subtract, AluOpType.mult, AluOpType.max
-SHR, AND, EQ = AluOpType.arith_shift_right, AluOpType.bitwise_and, AluOpType.is_equal
+ADD, SUB, MUL, MAX, MIN = AluOpType.add, AluOpType.subtract, AluOpType.mult, AluOpType.max, AluOpType.min
+
+
+def bits(engines):
+    return sum(1 << e for e in engines)
 
 
 def rank_program(g, core, T, topo):
@@ -38,18 +39,15 @@ def rank_program(g, core, T, topo):
     if rank is None:
         return
     V, S, P, Y = g.vector, g.scalar, g.tensor, g.sync
-    Copy, Ident = ActivationFunctionType.Copy, ActivationFunctionType.Identity
+    Copy = ActivationFunctionType.Copy
     chips = [topo.chip(c) for c in T.cores]
     steps = sorted([1, 3, 2], key=lambda v: 1 if topo.same_plane(chips[0], chips[v]) else 0)
     part = [rank ^ v for v in steps]
-    addr, mask, ne = [], [], []
-    for p in part:
-        a = topo.addr(T.cores[p])
-        addr.append((a[0], a[1]))
-        mask.append(topo.mask(core, T.cores[p]))
-        ne.append(len(topo.engines(core, T.cores[p])))
+    addr = [topo.addr(T.cores[p]) for p in part]
+    eng = [topo.engines(core, T.cores[p]) for p in part]
     dsts = [DstId(rid=a[0], pnc=a[1]) for a in addr]
-    both = mask[0] & mask[1] & mask[2]
+    both = [e for e in eng[0] if e in eng[1] and e in eng[2]]
+    ne, h = len(both), len(both) // 2
 
     cnt, seen = {}, {}
 
@@ -81,105 +79,104 @@ def rank_program(g, core, T, topo):
     t_xb = done(Y.dma_start(T.xw[:, XA:4 * XC], T.x[:, XA:4 * XC]), "ldxb", 16)
     t_qw = done(Y.dma_start(T.qt[:], T.qw[:]), "ldqw", 16)
 
-    i_p = done(g.iota(T.pi[:], [[0, 1]], 0, 1), "gi")
-    i_u4 = done(g.iota(T.u4[:], [[0, KO], [1, 4]], 0, 0, allow_small_or_imprecise_dtypes=True), "gi")
-    i_u16 = done(g.iota(T.u16[:], [[0, 8], [1, 16]], 0, 0, allow_small_or_imprecise_dtypes=True), "gi")
-    vneed(i_p)
-    v(V.tensor_scalar(T.lani[:, 0:1], T.pi[:], 2, 3, SHR, AND))
-    t = v(V.tensor_scalar(T.lani[:, 1:2], T.pi[:], 3, None, AND))
-    v(V.memset(T.ST[:, 128:136], 0.0))
-    vneed(t)
-    t = v(V.tensor_copy(T.lanf[:], T.lani[:]))
-    vneed(t, i_u4)
-    v(V.tensor_scalar(T.ul1[:], T.lanf[:, 0:1], 1.0, None, ADD))
-    v(V.tensor_scalar(T.suba[:], T.lanf[:, 0:1], 3.0, HOLD, AluOpType.is_lt, MUL))
-    t = v(V.tensor_scalar(T.dza[:], T.u4[:], 0.0, -4.0 * RAMP, EQ, MUL))
-    vneed(t)
-    v(V.tensor_scalar(T.subb[:], T.lanf[:, 0:1], RAMP, T.suba[:], MUL, ADD))
-    v(V.tensor_scalar(T.A[:], T.u4[:], T.ul1[:], HOLD, EQ, MUL))
-    t = v(V.tensor_scalar(T.dz[:], T.dza[:], RAMP + 4.0, None, ADD))
+    def iota(out, pattern, base=0):
+        return done(g.iota(out, pattern, base, 0, allow_small_or_imprecise_dtypes=True), "gi")
+
+    iota(T.lrow[:, 0:32], [[0, 2], [4, 16]])
+    iota(T.lrow[:, 32:64], [[0, 2], [2 * HOLD, 4], [0, 4]])
+    i_row = iota(T.lrow[:, 64:96], [[0, 2], [-HOLD, 4], [-1, 4]], 3 * HOLD)
+    i_u16 = iota(T.u16[:], [[0, 4], [4, 16]])
+    i_pc = iota(T.pc[:], [[64, 2], [1, 4]])
+    i_u4 = iota(T.u4[:], [[0, KO], [2 * HOLD, 4]], -HOLD)
+    lane4, turn, sub = T.lcol[:, 0:1], T.lcol[:, 32:33], T.lcol[:, 64:65]
+
+    v(V.memset(T.D[:], 0.0))
+    v(V.memset(T.xw[:, 4 * XC:4 * (XC + CAP)], 0.0))
+    v(V.memset(T.ST[:, 64:72], 0.0))
+    vneed(i_row)
+    t = v(V.transpose(T.lcol[:], T.lrow[:]))
+    v(V.memset(T.four[:], 4.0))
     vneed(t, i_u16)
-    v(V.tensor_scalar(T.sub[:], T.subb[:], T.lanf[:, 1:2], None, SUB))
-    v(V.tensor_scalar(T.A[:, 0:CAP:4], T.u4[:, 0:CAP:4], 0.0, DROP, MUL, ADD))
-    v(V.memset(T.dz[:, 0:1], 0.0))
-    t_const = v(V.tensor_scalar(T.resm[:], T.u16[:], 0.0, None, AluOpType.is_gt))
+    v(V.tensor_scalar(T.tri[:], T.u16[:], lane4, None, AluOpType.is_le))
+    v(V.tensor_scalar(T.resm[:], T.u16[:], 0.0, None, AluOpType.is_gt))
+    vneed(i_pc)
+    t_po = v(V.tensor_scalar(T.po[:], T.pc[:], lane4, None, ADD))
+    vneed(i_u4)
+    t_a = v(V.tensor_scalar(T.A[:], T.u4[:], turn, float(HOLD), SUB, MIN))
 
     vneed(t_cd)
     t = v(V.tensor_copy(T.cds[:], T.cdl[:]))
     need("g", g, t)
-    g.remote_dma_fused([RemoteDMATransfer(dst_ids=dsts, dma_engine_mask=both, remote_sem=T.sem.lst, srcs=[T.cds[:]],
+    g.remote_dma_fused([RemoteDMATransfer(dst_ids=dsts, dma_engine_mask=bits(both), remote_sem=T.sem.lst, srcs=[T.cds[:]],
                                           dsts=[T.lst[:, 4 * s:4 * s + 4] for s in range(3)])], local_sem=T.sem.snt)
-    nsent = ne[0]
+    nsent = ne
     g.sem_inc(T.sem.go, 1)
     need("g", g, t_tab)
     i_bc = done(g.partition_broadcast(T.bc[:], T.row[0:1, :], 128), "gi")
 
-    v(V.tensor_copy(T.lo[:, 6:7], T.cdl[:, rank:rank + 1]))
-    v(V.tensor_copy(T.lo[:, 7:8], T.cdl[:, rank:rank + 1]))
-    t_d = v(V.memset(T.D[:], 0.0))
-
-    vneed(i_bc)
-    for h in range(4):
-        t = v(V.tensor_copy(T.wn[:, 64 + 16 * h:80 + 16 * h], T.bc[:, 64 + h:128:4]))
-    for h in range(4):
-        t_wn = v(V.tensor_scalar(T.wn[:, 16 * h:16 + 16 * h], T.bc[:, h:64:4], 4.0, None, MUL))
-    vneed(t)
-    t = v(V.transpose(T.lnt[:], T.wn[:, 64:128]))
-    t_nl = v(V.tensor_scalar(T.nl[:], T.wn[:, 64:128], -4.0, None, MUL))
-    vneed(t)
-    t_lnb = v(V.tensor_copy(T.lnb[:], T.lnt[:, 0:64:32]))
-    vneed(t_wn, t_nl)
-    t_nen = v(V.tensor_tensor(T.nen[:], T.nl[:], T.wn[:, 0:64], SUB))
-
-    need("g", g, t_lnb)
-    g.remote_dma_fused([RemoteDMATransfer(dst_ids=dsts, dma_engine_mask=both, remote_sem=T.sem.lnarr, srcs=[T.lnb[:]],
-                                          dsts=[T.lnr[:, 2 * s:2 * s + 2] for s in range(3)])], local_sem=T.sem.snt)
-    nsent += ne[0]
-
-    t_tail = v(V.memset(T.xw[:, 4 * XC:4 * (XC + CAP)], 0.0))
-    v(V.memset(T.zer[:], 0.0))
+    v(V.tensor_copy(T.lo[:, 3:4], T.cdl[:, rank:rank + 1]))
+    vneed(t_a)
+    t_const = v(V.memset(T.A[:, 0:CAP:4], -8.0 * HOLD))
+    v(V.memset(T.mask[:], 0.0))
     v(V.memset(T.neg[:], LOW))
-    v(V.memset(T.Z[:, 0:4 * WIN:WIN], 0.0))
-    t_z = v(V.memset(T.mask[:], 0.0))
+    t_z = v(V.memset(T.Z[:, 0:4 * WIN:WIN], 0.0))
 
-    vneed(("lst", sum(ne)))
-    v(V.tensor_copy(T.lo[:, 0:6:2], T.lst[:, rank:12:4]))
-    t_lo = v(V.tensor_copy(T.lo[:, 1:6:2], T.lst[:, rank:12:4]))
+    vneed(i_bc, t_po)
+    t_ln = v(V.tensor_copy(T.lnw[:], T.bc[:].indirect(T.po[:, 4:8])))
+    t_stw = v(V.tensor_scalar(T.stw[:], T.bc[:].indirect(T.po[:, 0:4]), 4.0, -4.0, MUL, ADD))
+    vneed(t_ln)
+    t = v(V.tensor_scalar(T.nl[:], T.lnw[:], -4.0, None, MUL))
+    vneed(t_stw, t)
+    t_nen = v(V.tensor_tensor(T.nen[:], T.nl[:], T.stw[:], SUB))
+
+    vneed(("lst", 3 * ne))
+    t_lo = v(V.tensor_copy(T.lo[:, 0:3], T.lst[:, rank:12:4]))
     need("s", S, t_lo)
-    t_st = done(S.activation(T.ST[:, 0:128], T.wn[:, 0:64].indirect(T.lo[:]), Copy), "s")
+    t_st = done(S.activation(T.ST[:, 0:64], T.stw[:].indirect(T.lo[:]), Copy), "s")
     vneed(t_lo)
-    t = v(V.tensor_copy(T.G[:], T.wn[:, 64:128].indirect(T.lo[:])))
+    t = v(V.tensor_tensor(T.MG[:], T.lnw[:].indirect(T.lo[:]), T.tri[:], MUL))
     vneed(t)
-    t = v(V.tensor_tensor_scan(T.C[:], T.resm[:], T.G[:], 0.0, MUL, ADD))
+    t = v(V.tensor_tensor_scan(T.C[:], T.resm[:], T.MG[:], 0.0, MUL, ADD))
+    vneed(t_st, t_nen)
+    v(V.tensor_tensor(T.J[:], T.nen[:].indirect(T.lo[:]), T.ST[:, 1:65], ADD))
     vneed(t)
-    t = v(V.transpose(T.TR[:], T.C[:]))
-    vneed(t)
-    t_c = v(V.tensor_copy(T.cL[:, 0:8:2], T.TR[:, 0:128:32]))
-    vneed(t_st)
-    t_j = v(V.tensor_tensor(T.J[:], T.nen[:].indirect(T.lo[:]), T.ST[:, 1:129], ADD))
+    t_c = v(V.tensor_copy(T.cL[:, 0:8:2], T.C[:, 15:64:16]))
 
-    def chain(k):
-        a, c = 32 * k, CAP * k
-        vneed(t_j, t_c, t_d, t_tail)
-        t = v(V.tensor_copy(T.D[:, WIN * k:WIN * k + CAP + 1].indirect(T.cL[:, 2 * k:2 * k + 1]), T.J[:, a:a + 16]))
+    need("g", g, t_c)
+    share = [both[:h], both[h:h + h // 2], both[h + h // 2:]]
+    g.remote_dma_fused([RemoteDMATransfer(dst_ids=[dsts[s]], dma_engine_mask=bits(share[s]), remote_sem=T.sem.sel,
+                                          srcs=[T.cL[:, 2 * s:2 * s + 1]], dsts=[T.seL[:, 2 * s:2 * s + 1]])
+                        for s in range(3)], local_sem=T.sem.snt)
+    nsent += ne
+
+    def jumps(k):
+        vneed(t_c)
+        return v(V.tensor_copy(T.D[:, WIN * k:WIN * k + CAP + 1].indirect(T.cL[:, 2 * k:2 * k + 1]), T.J[:, 16 * k:16 * k + 16]))
+
+    def run(k, t):
         vneed(t)
-        t = v(V.tensor_tensor_scan(T.SS[:, c:c + CAP], T.dz[:], T.D[:, WIN * k:WIN * k + CAP], T.ST[:, a:a + 1], ADD, ADD))
+        return v(V.tensor_tensor_scan(T.SS[:, CAP * k:CAP * k + CAP], T.four[:], T.D[:, WIN * k:WIN * k + CAP],
+                                      T.ST[:, 16 * k:16 * k + 1], ADD, ADD))
+
+    def hold(k, t):
         vneed(t)
-        t = v(V.tensor_tensor_scan(T.XX[:, c:c + CAP], T.A[:], T.SS[:, c:c + CAP], 0.0, ADD, MAX))
+        return v(V.tensor_tensor_scan(T.XX[:, CAP * k:CAP * k + CAP], T.A[:], T.SS[:, CAP * k:CAP * k + CAP], 0.0, ADD, MAX))
+
+    def offsets(k, t):
         vneed(t)
-        return v(V.tensor_scalar(T.O[:, KO * k:KO * k + KO], T.XX[:, c + 3:c + CAP:4], T.sub[:], None, SUB))
+        return v(V.tensor_scalar(T.O[:, KO * k:KO * k + KO], T.XX[:, CAP * k + 3:CAP * k + CAP:4], sub, None, SUB))
 
     def piece(k, a, b):
         return (T.tile[:, 4 * CAP * k + 16 * a:4 * CAP * k + 16 * b], T.xw[:].indirect(T.O[:, KO * k + a:KO * k + b]))
 
-    def gather_s(k, cut, t_o):
+    def gather_s(k, t_o):
         need("s", S, t_o, t_xa, t_xb)
-        o, i = piece(k, cut, KO)
+        o, i = piece(k, CUT, KO)
         return done(S.activation(o, i, Copy), "s")
 
-    def gather_v(k, cut, t_o):
+    def gather_v(k, t_o):
         vneed(t_o, t_xa, t_xb)
-        o, i = piece(k, 0, cut)
+        o, i = piece(k, 0, CUT)
         return v(V.tensor_copy(o, i))
 
     def quant(k, *toks):
@@ -187,65 +184,79 @@ def rank_program(g, core, T, topo):
         return v(V.quantize_mx(T.qc[:, CAP * k:CAP * k + CAP], T.qs[:, CAP * k:CAP * k + CAP],
                                T.tile[:, 4 * CAP * k:4 * CAP * (k + 1)]))
 
-    def send(s, t):
+    def send_codes(s, t):
         need("g", g, t)
         lo, hi = CAP * s, CAP * s + CAP
         g.remote_dma(T.lc[:, lo:hi].bitcast(dt.uint8), T.qc[:, lo:hi].bitcast(dt.uint8), T.sem["arr%d" % s], T.sem.snt,
-                     addr[s][1], addr[s][0], mask[s])
-        g.remote_dma(T.lp[:, lo:hi], T.qs[:, lo:hi], T.sem["arr%d" % s], T.sem.snt,
-                     addr[s][1], addr[s][0], mask[s])
-        return 2 * ne[s]
+                     addr[s][1], addr[s][0], bits(both))
+        return ne
 
-    t_o = [chain(0), chain(1), chain(2)]
-    for s in range(3):
-        t_s = gather_s(s, 18, t_o[s])
-        t_v = gather_v(s, 18, t_o[s])
-        nsent += send(s, quant(s, t_v, t_s))
+    a0 = jumps(0)
+    a1 = jumps(1)
+    b0 = run(0, a0)
+    a2 = jumps(2)
+    c0 = hold(0, b0)
+    b1 = run(1, a1)
+    o0 = offsets(0, c0)
+    c1 = hold(1, b1)
+    b2 = run(2, a2)
+    o1 = offsets(1, c1)
+    c2 = hold(2, b2)
+    s0 = gather_s(0, o0)
+    s1 = gather_s(1, o1)
+    o2 = offsets(2, c2)
+    s2 = gather_s(2, o2)
+    v0 = gather_v(0, o0)
+    nsent += send_codes(0, quant(0, v0, s0))
+    v1 = gather_v(1, o1)
+    nsent += send_codes(1, quant(1, v1, s1))
+    g.remote_dma_fused([RemoteDMATransfer(dst_ids=[dsts[s]], dma_engine_mask=bits(both[h * s:h * s + h]),
+                                          remote_sem=T.sem["arr%d" % s], srcs=[T.qs[:, CAP * s:CAP * s + CAP]],
+                                          dsts=[T.lp[:, CAP * s:CAP * s + CAP]]) for s in range(2)], local_sem=T.sem.snt)
+    nsent += ne
+    v2 = gather_v(2, o2)
+    nsent += send_codes(2, quant(2, v2, s2))
+    g.remote_dma(T.lp[:, 2 * CAP:3 * CAP], T.qs[:, 2 * CAP:3 * CAP], T.sem.arr2, T.sem.snt, addr[2][1], addr[2][0], bits(both))
+    nsent += ne
+    n_arr = [ne + h, ne + h, 2 * ne]
 
-    t_o3 = chain(3)
-    v(V.tensor_copy(T.cdo[:, 0:8:2], T.cdl[:]))
-    t_cdo = v(V.tensor_copy(T.cdo[:, 1:8:2], T.cdl[:]))
+    def ends(k):
+        return T.cL[:, 6:7] if k == 3 else T.seL[:, 2 * k:2 * k + 1]
+
+    def marks(k):
+        vneed(t_z)
+        return v(V.tensor_copy(T.mask[:, WIN * k:WIN * k + CAP + 1].indirect(ends(k)), T.neg[:]))
+
+    t_mk = {}
+    a3 = jumps(3)
+    t_mk[3] = marks(3)
+    b3 = run(3, a3)
     vneed(t_qw)
     t_q = v(V.quantize_mx(T.qwc[:], T.qws[:], T.qt[:]))
-    need("s", S, ("lnarr", sum(ne)), t_z)
-    for n in range(6):
-        t = done(S.activation(T.wb2[:, 32 * n:32 * n + 32], T.zer[:], Ident, bias=T.lnr[:, n:n + 1]), "s")
-    t_g3 = gather_s(3, 0, t_o3)
-    vneed(t, t_cdo, t_z)
-    t_m3 = v(V.tensor_copy(T.mask[:, WIN * 3:WIN * 3 + CAP + 1].indirect(T.cL[:, 6:7]), T.neg[:]))
-    t = v(V.transpose(T.wn2[:], T.wb2[:]))
-    vneed(t)
-    for s in range(3):
-        p = part[s]
-        t = v(V.tensor_copy(T.G2[:, 32 * s:32 * s + 32], T.wn2[:, 64 * s:64 * s + 64].indirect(T.cdo[:, 2 * p:2 * p + 2])))
-    vneed(t)
-    t = v(V.tensor_tensor_scan(T.C2[:], T.resm[:, 0:96], T.G2[:], 0.0, MUL, ADD))
-    vneed(t)
-    t = v(V.transpose(T.TR2[:], T.C2[:]))
-    vneed(t)
-    t_se = v(V.tensor_copy(T.seL[:, 0:6:2], T.TR2[:, 0:96:32]))
-    vneed(t_se)
-    t_mk = []
-    for s in range(3):
-        t_mk.append(v(V.tensor_copy(T.mask[:, WIN * s:WIN * s + CAP + 1].indirect(T.seL[:, 2 * s:2 * s + 1]), T.neg[:])))
-    t_q3 = quant(3, t_g3)
+    c3 = hold(3, b3)
+    vneed(("sel", ne))
+    t_mk[0] = marks(0)
+    o3 = offsets(3, c3)
+    t_mk[1] = marks(1)
+    s3 = gather_s(3, o3)
+    v3 = gather_v(3, o3)
+    t_mk[2] = marks(2)
+    t_q3 = quant(3, v3, s3)
 
     need("p", P, t_q)
     for k in (3, 0, 1, 2):
         if k == 3:
             need("p", P, t_q3)
-            rc, rp = T.qc[:, 3 * CAP:4 * CAP], T.qs[:, 3 * CAP:4 * CAP]
-            q, ends, t_mask = rank, T.cL[:, 6:7], t_m3
+            rc, rp, q = T.qc[:, 3 * CAP:4 * CAP], T.qs[:, 3 * CAP:4 * CAP], rank
         else:
-            need("p", P, ("arr%d" % k, 2 * ne[k]))
-            rc, rp = T.lc[:, CAP * k:CAP * k + CAP], T.lp[:, CAP * k:CAP * k + CAP]
-            q, ends, t_mask = part[k], T.seL[:, 2 * k:2 * k + 1], t_mk[k]
+            need("p", P, ("arr%d" % k, n_arr[k]))
+            rc, rp, q = T.lc[:, CAP * k:CAP * k + CAP], T.lp[:, CAP * k:CAP * k + CAP], part[k]
         t = done(P.matmul_mx(T.ps[:, 512 * k:512 * k + CAP], T.qwc[:], T.qws[:], rc, rp, True, True), "pe")
-        vneed(t, t_mask)
+        vneed(t, t_mk[k])
         t = v(V.tensor_tensor_scan(T.Z[:, WIN * k + 1:WIN * k + 1 + CAP], T.mask[:, WIN * k:WIN * k + CAP],
                                    T.ps[:, 512 * k:512 * k + CAP], LOW, ADD, MAX))
         vneed(t)
-        t = v(V.tensor_copy(T.yo[:, CD * q:CD * q + CD], T.Z[:, WIN * k:WIN * k + CAP + 1].indirect(ends)))
+        t = v(V.tensor_copy(T.yo[:, CD * q:CD * q + CD], T.Z[:, WIN * k:WIN * k + CAP + 1].indirect(ends(k))))
         need("y", Y, t)
         done(Y.dma_start(T.y[:, CD * q:CD * q + CD], T.yo[:, CD * q:CD * q + CD]), "yst", 16)
     need("y", Y, ("yst", 64))

import numpy as np
from concourse.bass import DstId, RemoteDMATransfer
from concourse.mybir import dt, AluOpType, ActivationFunctionType

CAP = 144
WIN = 152
KO = CAP // 4
ND, CD, XC = 64, 16, 1024
XA = 1408
CUT = 16
LOW = -1.0e29
HOLD = 8192

F, I, U, B = "float32", "int32", "uint16", "bfloat16"
SCRATCH = {n: ("sbuf", [128, w], d) for n, w, d in [
    ("xw", 4 * (XC + CAP), B), ("qt", 512, B), ("tile", 16 * CAP, B),
    ("qwc", 128, "float8_e4m3fn_x4"), ("qws", 128, "uint8"), ("qc", 4 * CAP, "float8_e4m3fn_x4"), ("qs", 4 * CAP, "uint8"),
    ("lc", 3 * CAP, "float8_e4m3fn_x4"), ("lp", 3 * CAP, "uint8"),
    ("cdl", 4, I), ("cds", 4, U), ("lst", 12, U), ("lo", 4, U),
    ("row", 128, I), ("bc", 128, I), ("stw", 64, F), ("lnw", 64, F), ("nl", 64, F), ("nen", 64, F),
    ("MG", 64, F), ("C", 64, F), ("ST", 72, F), ("J", 64, F), ("cL", 8, U), ("seL", 6, U),
    ("D", 4 * WIN, F), ("SS", 4 * CAP, F), ("XX", 4 * CAP, F), ("O", CAP, U),
    ("mask", 4 * WIN, F), ("Z", 4 * WIN, F), ("yo", 64, F), ("neg", 16, F),
    ("lrow", 96, F), ("lcol", 96, F), ("u16", 64, F), ("u4", CAP, F), ("pc", 8, F), ("po", 8, U),
    ("tri", 64, F), ("resm", 64, F), ("A", CAP, F), ("four", CAP, F)]}
SCRATCH["ps"] = ("psum", [128, 2048], F)
SEMAPHORES = ["ldcd", "ldtab", "ldqw", "ldxa", "ldxb", "v", "s", "pe", "gi", "go", "lst", "sel",
              "arr0", "arr1", "arr2", "snt", "yst"]

ADD, SUB, MUL, MAX, MIN = AluOpType.add, AluOpType.subtract, AluOpType.mult, AluOpType.max, AluOpType.min


def bits(engines):
    return sum(1 << e for e in engines)


def rank_program(g, core, T, topo):
    rank = T.rank_of(core)
    if rank is None:
        return
    V, S, P, Y = g.vector, g.scalar, g.tensor, g.sync
    Copy = ActivationFunctionType.Copy
    chips = [topo.chip(c) for c in T.cores]
    steps = sorted([1, 3, 2], key=lambda v: 1 if topo.same_plane(chips[0], chips[v]) else 0)
    part = [rank ^ v for v in steps]
    addr = [topo.addr(T.cores[p]) for p in part]
    eng = [topo.engines(core, T.cores[p]) for p in part]
    dsts = [DstId(rid=a[0], pnc=a[1]) for a in addr]
    both = [e for e in eng[0] if e in eng[1] and e in eng[2]]
    ne, h = len(both), len(both) // 2

    cnt, seen = {}, {}

    def done(ins, name, n=1):
        ins.then_inc(T.sem[name], n)
        cnt[name] = cnt.get(name, 0) + n
        return (name, cnt[name])

    def need(qn, q, *toks):
        for name, val in toks:
            if seen.get((qn, name), 0) < val:
                q.wait_ge(T.sem[name], val)
                seen[(qn, name)] = val

    def vneed(*toks):
        need("v", V, *toks)

    def v(ins):
        return done(ins, "v")

    for k in range(8):
        q = Y if k < 4 else S
        done(q.dma_start(T.cdl[16 * k:16 * k + 16, :], T.cd[:]), "ldcd", 16)
    done(S.dma_start(T.row[0:1, 0:64], T.st[:]), "ldtab", 16)
    done(S.dma_start(T.row[0:1, 64:128], T.ln[:]), "ldtab", 16)
    t_cd, t_tab = ("ldcd", 128), ("ldtab", 32)
    t_xa = done(Y.dma_start(T.xw[:, 0:XA], T.x[:, 0:XA]), "ldxa", 16)
    Y.wait_ge(T.sem.go, 1)
    t_xb = done(Y.dma_start(T.xw[:, XA:4 * XC], T.x[:, XA:4 * XC]), "ldxb", 16)
    t_qw = done(Y.dma_start(T.qt[:], T.qw[:]), "ldqw", 16)

    def iota(out, pattern, base=0):
        return done(g.iota(out, pattern, base, 0, allow_small_or_imprecise_dtypes=True), "gi")

    iota(T.lrow[:, 0:32], [[0, 2], [4, 16]])
    iota(T.lrow[:, 32:64], [[0, 2], [2 * HOLD, 4], [0, 4]])
    i_row = iota(T.lrow[:, 64:96], [[0, 2], [-HOLD, 4], [-1, 4]], 3 * HOLD)
    i_u16 = iota(T.u16[:], [[0, 4], [4, 16]])
    i_pc = iota(T.pc[:], [[64, 2], [1, 4]])
    i_u4 = iota(T.u4[:], [[0, KO], [2 * HOLD, 4]], -HOLD)
    lane4, turn, sub = T.lcol[:, 0:1], T.lcol[:, 32:33], T.lcol[:, 64:65]

    v(V.memset(T.D[:], 0.0))
    v(V.memset(T.xw[:, 4 * XC:4 * (XC + CAP)], 0.0))
    v(V.memset(T.ST[:, 64:72], 0.0))
    vneed(i_row)
    t = v(V.transpose(T.lcol[:], T.lrow[:]))
    v(V.memset(T.four[:], 4.0))
    vneed(t, i_u16)
    v(V.tensor_scalar(T.tri[:], T.u16[:], lane4, None, AluOpType.is_le))
    v(V.tensor_scalar(T.resm[:], T.u16[:], 0.0, None, AluOpType.is_gt))
    vneed(i_pc)
    t_po = v(V.tensor_scalar(T.po[:], T.pc[:], lane4, None, ADD))
    vneed(i_u4)
    t_a = v(V.tensor_scalar(T.A[:], T.u4[:], turn, float(HOLD), SUB, MIN))

    vneed(t_cd)
    t = v(V.tensor_copy(T.cds[:], T.cdl[:]))
    need("g", g, t)
    g.remote_dma_fused([RemoteDMATransfer(dst_ids=dsts, dma_engine_mask=bits(both), remote_sem=T.sem.lst, srcs=[T.cds[:]],
                                          dsts=[T.lst[:, 4 * s:4 * s + 4] for s in range(3)])], local_sem=T.sem.snt)
    nsent = ne
    g.sem_inc(T.sem.go, 1)
    need("g", g, t_tab)
    i_bc = done(g.partition_broadcast(T.bc[:], T.row[0:1, :], 128), "gi")

    v(V.tensor_copy(T.lo[:, 3:4], T.cdl[:, rank:rank + 1]))
    vneed(t_a)
    t_const = v(V.memset(T.A[:, 0:CAP:4], -8.0 * HOLD))
    v(V.memset(T.mask[:], 0.0))
    v(V.memset(T.neg[:], LOW))
    t_z = v(V.memset(T.Z[:, 0:4 * WIN:WIN], 0.0))

    vneed(i_bc, t_po)
    t_ln = v(V.tensor_copy(T.lnw[:], T.bc[:].indirect(T.po[:, 4:8])))
    t_stw = v(V.tensor_scalar(T.stw[:], T.bc[:].indirect(T.po[:, 0:4]), 4.0, -4.0, MUL, ADD))
    vneed(t_ln)
    t = v(V.tensor_scalar(T.nl[:], T.lnw[:], -4.0, None, MUL))
    vneed(t_stw, t)
    t_nen = v(V.tensor_tensor(T.nen[:], T.nl[:], T.stw[:], SUB))

    vneed(("lst", 3 * ne))
    t_lo = v(V.tensor_copy(T.lo[:, 0:3], T.lst[:, rank:12:4]))
    need("s", S, t_lo)
    t_st = done(S.activation(T.ST[:, 0:64], T.stw[:].indirect(T.lo[:]), Copy), "s")
    vneed(t_lo)
    t = v(V.tensor_tensor(T.MG[:], T.lnw[:].indirect(T.lo[:]), T.tri[:], MUL))
    vneed(t)
    t = v(V.tensor_tensor_scan(T.C[:], T.resm[:], T.MG[:], 0.0, MUL, ADD))
    vneed(t_st, t_nen)
    v(V.tensor_tensor(T.J[:], T.nen[:].indirect(T.lo[:]), T.ST[:, 1:65], ADD))
    vneed(t)
    t_c = v(V.tensor_copy(T.cL[:, 0:8:2], T.C[:, 15:64:16]))

    need("g", g, t_c)
    share = [both[:h], both[h:h + h // 2], both[h + h // 2:]]
    g.remote_dma_fused([RemoteDMATransfer(dst_ids=[dsts[s]], dma_engine_mask=bits(share[s]), remote_sem=T.sem.sel,
                                          srcs=[T.cL[:, 2 * s:2 * s + 1]], dsts=[T.seL[:, 2 * s:2 * s + 1]])
                        for s in range(3)], local_sem=T.sem.snt)
    nsent += ne

    def jumps(k):
        vneed(t_c)
        return v(V.tensor_copy(T.D[:, WIN * k:WIN * k + CAP + 1].indirect(T.cL[:, 2 * k:2 * k + 1]), T.J[:, 16 * k:16 * k + 16]))

    def run(k, t):
        vneed(t)
        return v(V.tensor_tensor_scan(T.SS[:, CAP * k:CAP * k + CAP], T.four[:], T.D[:, WIN * k:WIN * k + CAP],
                                      T.ST[:, 16 * k:16 * k + 1], ADD, ADD))

    def hold(k, t):
        vneed(t)
        return v(V.tensor_tensor_scan(T.XX[:, CAP * k:CAP * k + CAP], T.A[:], T.SS[:, CAP * k:CAP * k + CAP], 0.0, ADD, MAX))

    def offsets(k, t):
        vneed(t)
        return v(V.tensor_scalar(T.O[:, KO * k:KO * k + KO], T.XX[:, CAP * k + 3:CAP * k + CAP:4], sub, None, SUB))

    def piece(k, a, b):
        return (T.tile[:, 4 * CAP * k + 16 * a:4 * CAP * k + 16 * b], T.xw[:].indirect(T.O[:, KO * k + a:KO * k + b]))

    def gather_s(k, t_o):
        need("s", S, t_o, t_xa, t_xb)
        o, i = piece(k, CUT, KO)
        return done(S.activation(o, i, Copy), "s")

    def gather_v(k, t_o):
        vneed(t_o, t_xa, t_xb)
        o, i = piece(k, 0, CUT)
        return v(V.tensor_copy(o, i))

    def quant(k, *toks):
        vneed(*toks)
        return v(V.quantize_mx(T.qc[:, CAP * k:CAP * k + CAP], T.qs[:, CAP * k:CAP * k + CAP],
                               T.tile[:, 4 * CAP * k:4 * CAP * (k + 1)]))

    def send_codes(s, t):
        need("g", g, t)
        lo, hi = CAP * s, CAP * s + CAP
        g.remote_dma(T.lc[:, lo:hi].bitcast(dt.uint8), T.qc[:, lo:hi].bitcast(dt.uint8), T.sem["arr%d" % s], T.sem.snt,
                     addr[s][1], addr[s][0], bits(both))
        return ne

    a0 = jumps(0)
    a1 = jumps(1)
    b0 = run(0, a0)
    a2 = jumps(2)
    c0 = hold(0, b0)
    b1 = run(1, a1)
    o0 = offsets(0, c0)
    c1 = hold(1, b1)
    b2 = run(2, a2)
    o1 = offsets(1, c1)
    c2 = hold(2, b2)
    s0 = gather_s(0, o0)
    s1 = gather_s(1, o1)
    o2 = offsets(2, c2)
    s2 = gather_s(2, o2)
    v0 = gather_v(0, o0)
    nsent += send_codes(0, quant(0, v0, s0))
    v1 = gather_v(1, o1)
    nsent += send_codes(1, quant(1, v1, s1))
    g.remote_dma_fused([RemoteDMATransfer(dst_ids=[dsts[s]], dma_engine_mask=bits(both[h * s:h * s + h]),
                                          remote_sem=T.sem["arr%d" % s], srcs=[T.qs[:, CAP * s:CAP * s + CAP]],
                                          dsts=[T.lp[:, CAP * s:CAP * s + CAP]]) for s in range(2)], local_sem=T.sem.snt)
    nsent += ne
    v2 = gather_v(2, o2)
    nsent += send_codes(2, quant(2, v2, s2))
    g.remote_dma(T.lp[:, 2 * CAP:3 * CAP], T.qs[:, 2 * CAP:3 * CAP], T.sem.arr2, T.sem.snt, addr[2][1], addr[2][0], bits(both))
    nsent += ne
    n_arr = [ne + h, ne + h, 2 * ne]

    def ends(k):
        return T.cL[:, 6:7] if k == 3 else T.seL[:, 2 * k:2 * k + 1]

    def marks(k):
        vneed(t_z)
        return v(V.tensor_copy(T.mask[:, WIN * k:WIN * k + CAP + 1].indirect(ends(k)), T.neg[:]))

    t_mk = {}
    a3 = jumps(3)
    t_mk[3] = marks(3)
    b3 = run(3, a3)
    vneed(t_qw)
    t_q = v(V.quantize_mx(T.qwc[:], T.qws[:], T.qt[:]))
    c3 = hold(3, b3)
    vneed(("sel", ne))
    t_mk[0] = marks(0)
    o3 = offsets(3, c3)
    t_mk[1] = marks(1)
    s3 = gather_s(3, o3)
    v3 = gather_v(3, o3)
    t_mk[2] = marks(2)
    t_q3 = quant(3, v3, s3)

    need("p", P, t_q)
    for k in (3, 0, 1, 2):
        if k == 3:
            need("p", P, t_q3)
            rc, rp, q = T.qc[:, 3 * CAP:4 * CAP], T.qs[:, 3 * CAP:4 * CAP], rank
        else:
            need("p", P, ("arr%d" % k, n_arr[k]))
            rc, rp, q = T.lc[:, CAP * k:CAP * k + CAP], T.lp[:, CAP * k:CAP * k + CAP], part[k]
        t = done(P.matmul_mx(T.ps[:, 512 * k:512 * k + CAP], T.qwc[:], T.qws[:], rc, rp, True, True), "pe")
        vneed(t, t_mk[k])
        t = v(V.tensor_tensor_scan(T.Z[:, WIN * k + 1:WIN * k + 1 + CAP], T.mask[:, WIN * k:WIN * k + CAP],
                                   T.ps[:, 512 * k:512 * k + CAP], LOW, ADD, MAX))
        vneed(t)
        t = v(V.tensor_copy(T.yo[:, CD * q:CD * q + CD], T.Z[:, WIN * k:WIN * k + CAP + 1].indirect(ends(k))))
        need("y", Y, t)
        done(Y.dma_start(T.y[:, CD * q:CD * q + CD], T.yo[:, CD * q:CD * q + CD]), "yst", 16)
    need("y", Y, ("yst", 64))
    need("g", g, ("snt", nsent))
